import numpy as np
import ml_dtypes


def mxq(x, axis, fmt="e4m3"):
    dtype, down = {"e4m3": (ml_dtypes.float8_e4m3fn, 7), "e5m2": (ml_dtypes.float8_e5m2, 14)}[fmt]
    v = np.moveaxis(np.asarray(x, np.float32).astype(ml_dtypes.bfloat16).astype(np.float64), axis, -1)
    blocks = v.reshape(v.shape[:-1] + (-1, 32))
    amax = np.abs(blocks).max(-1, keepdims=True)
    byte = np.maximum(np.where(amax > 0, np.frexp(amax)[1] - 1 + 127, 0) - down, 1)
    scale = np.exp2(byte - 127.0)
    codes = (blocks / scale).astype(np.float32).astype(dtype).astype(np.float64)
    return np.moveaxis((codes * scale).reshape(v.shape), -1, axis)


WIDE = False


def mx_kscale(k):
    if not WIDE:
        return np.ones(k)
    levels = np.array([10, -10, 5, -5, 0])
    if k % 512:
        return np.exp2(np.random.permutation(np.resize(levels, k // 32))).repeat(32)
    a = np.empty((k // 512, 16))
    for p in range(k // 512):
        a[p, :8] = np.random.permutation(np.resize(levels, 8))
        for g in range(8):
            far = levels[np.abs(levels - a[p, g]) >= 10]
            a[p, g + 8] = far[np.random.randint(len(far))]
    return np.exp2(a.ravel()).repeat(32)


def f64(x):
    return np.asarray(x).astype(np.float64)


def striped(idx):
    return np.tile(idx.reshape(-1, 16).T, (8, 1)).astype(np.uint16)


def unstriped(offs):
    return offs[:16].T.reshape(-1).astype(np.int64)


def pack_weight(w):
    k, n = w.shape
    w = f64(np.asarray(w, np.float32).astype(ml_dtypes.bfloat16)).reshape(k // 32, 32, n)
    amax = np.abs(w).max(1)
    byte = np.clip(np.where(amax > 0, np.frexp(amax)[1] - 1 + 127 - 7, 1), 1, 254)
    scaled = (w * np.exp2(127.0 - byte)[:, None, :]).reshape(k, n).astype(np.float32)
    words = np.ascontiguousarray(scaled.reshape(k // 512, 128, 4, n).transpose(0, 1, 3, 2)).astype(ml_dtypes.float8_e4m3fn).view(np.uint8)
    return words, np.ascontiguousarray(byte.astype(np.uint8).reshape(k // 512, 16, n))


def unpack_weight(words, scales):
    g, p, n, _ = words.shape
    vals = np.ascontiguousarray(words).view(ml_dtypes.float8_e4m3fn).astype(np.float64) * np.repeat(np.exp2(scales.astype(np.float64) - 127.0), 8, axis=1)[..., None]
    return vals.transpose(0, 1, 3, 2).reshape(g * 512, n)


K, T, S, V, R = 512, 2048, 512, 512, 256


def setup_inputs():
    n = np.random.standard_normal
    s = mx_kscale(K)[:, None]
    packed_xT = pack_weight(n((K, T)) * s)
    return {
        "x_words": packed_xT[0],
        "x_scales": packed_xT[1],
        "hT": (n((K, V)) / np.sqrt(K) / s).astype(np.float32),
        "cnt": (np.floor(np.random.uniform(1.0, 4.0, (V, R)))).astype(np.float32),
        "offs": striped(np.random.permutation(T)[:S]),
        "hist": striped(np.random.permutation(S)[:R]),
    }


def reference(x_words, x_scales, hT, cnt, offs, hist):
    hTq = mxq(f64(hT), 0, "e4m3")
    xq = unpack_weight(x_words, x_scales)[:, unstriped(offs)]
    y = hTq.T @ xq
    gg = y[:, unstriped(hist)]
    z = y.copy()
    z[:, unstriped(hist)] = gg - (0.3 * f64(cnt) + 0.2)
    ex = np.exp(z - z.max(axis=1, keepdims=True))
    return ex / ex.sum(axis=1, keepdims=True)

@@ -1,0 +1,146 @@
+from contextlib import ExitStack
+
+import concourse.mybir as mybir
+
+K, T, S, V, R = 512, 2048, 512, 512, 256
+FLOPS = 2 * K * V * S
+
+F32 = mybir.dt.float32
+BF16 = mybir.dt.bfloat16
+I32 = mybir.dt.int32
+U32 = mybir.dt.uint32
+U16 = mybir.dt.uint16
+U8 = mybir.dt.uint8
+FP8X4 = mybir.dt.float8_e4m3fn_x4
+ACT = mybir.ActivationFunctionType
+ALU = mybir.AluOpType
+AXIS = mybir.AxisListType
+
+P = 128
+PACK = 4
+TILES = V // P
+HALF = S // 2
+
+
+def tile_picked_yrepp_pen_p_kernel(tc, x_words, x_scales, hT, cnt, offs, hist, out):
+    nc = tc.nc
+    with ExitStack() as ctx:
+        keep = ctx.enter_context(tc.tile_pool(name="keep", bufs=1))
+        psum = ctx.enter_context(tc.psum_pool(name="psum", bufs=1))
+
+        offs_sb = keep.tile([P, S // 16], U16, name="offs_sb")
+        hist_sb = keep.tile([P, R // 16], U16, name="hist_sb")
+        word_table = keep.tile([P, T], U32, name="word_table")
+        scale_table = keep.tile([P, T], U8, name="scale_table")
+        x_codes = keep.tile([P, S], U32, name="x_codes", align_bytes=64)
+        x_bytes = keep.tile([P, S], U8, name="x_bytes", align_bytes=64)
+
+        def per_tile(name, shape, dtype):
+            return [keep.tile(shape, dtype, name="%s%d" % (name, i), align_bytes=64) for i in range(TILES)]
+
+        h_raw = [keep.tile([P, PACK, 2 * P], F32, name="h_raw%d" % u) for u in range(2)]
+        h_bf = [keep.tile([P, 2 * P, PACK], BF16, name="h_bf%d" % u, align_bytes=64) for u in range(2)]
+        h_codes = [keep.tile([P, 2 * P], U32, name="h_codes%d" % u, align_bytes=64) for u in range(2)]
+        h_bytes = [keep.tile([P, 2 * P], U8, name="h_bytes%d" % u, align_bytes=64) for u in range(2)]
+        counts_first = keep.tile([P, R], F32, name="counts_first")
+        counts_rest = keep.tile([P, TILES - 1, R], F32, name="counts_rest")
+        counts = [counts_first[:]] + [counts_rest[:, i, :] for i in range(TILES - 1)]
+        drop = per_tile("drop", [P, R], F32)
+        z = per_tile("z", [P, S], F32)
+        slots = [keep.tile([P, R], F32, name="picked%d" % u) for u in range(2)]
+        picked = [slots[i % 2] for i in range(TILES)]
+        neg_max = per_tile("neg_max", [P, 1], F32)
+        total = [picked[i][:, 0:1] for i in range(TILES)]
+        inv = per_tile("inv", [P, 1], F32)
+        e = per_tile("e", [P, S], F32)
+        prob = per_tile("prob", [P, S], F32)
+
+        def load_h(u):
+            nc.sync.dma_start(
+                out=h_raw[u][:], in_=hT[:, 2 * u * P : 2 * (u + 1) * P].rearrange("(p j) w -> p j w", j=PACK)
+            )
+
+        def cast_views(u):
+            return (
+                h_bf[u][:].rearrange("p (c w) j -> p c j w", w=4),
+                h_raw[u][:].rearrange("p j (c w) -> p c j w", w=4),
+            )
+
+        def quantize_h(u):
+            nc.vector.quantize_mx(
+                out=h_codes[u][:].bitcast(FP8X4), scales=h_bytes[u][:], in_=h_bf[u][:].rearrange("p w j -> p (w j)")
+            )
+
+        def penalty(i):
+            nc.scalar.activation(out=drop[i][:], in_=counts[i], func=ACT.Copy, scale=-0.3, bias=-0.2)
+
+        def logits(i, lo, hi):
+            cols = slice((i % 2) * P, (i % 2 + 1) * P)
+            acc = psum.tile([P, hi - lo], F32, name="acc%d_%d" % (i, lo))
+            nc.tensor.matmul_mx(
+                out=acc[:],
+                lhsT=h_codes[i // 2][:, cols].bitcast(FP8X4),
+                lhsT_scale=h_bytes[i // 2][:, cols],
+                rhs=x_codes[:, lo:hi].bitcast(FP8X4),
+                rhs_scale=x_bytes[:, lo:hi],
+                start=True,
+                stop=True,
+            )
+            nc.scalar.activation(out=z[i][:, lo:hi], in_=acc[:], func=ACT.Copy)
+
+        def gather(i):
+            nc.vector.tensor_copy(out=picked[i][:], in_=z[i][:].indirect(hist_sb[:]))
+
+        def scatter(i):
+            nc.vector.tensor_tensor(out=z[i][:].indirect(hist_sb[:]), in0=picked[i][:], in1=drop[i][:], op=ALU.add)
+
+        def row_max(i):
+            nc.vector.tensor_reduce(out=neg_max[i][:], in_=z[i][:], axis=AXIS.X, op=ALU.max, negate=True)
+            nc.scalar.activation(out=e[i][:], in_=z[i][:], func=ACT.Exp, bias=neg_max[i][:], accum_out=total[i])
+
+        def finish(i):
+            nc.vector.reciprocal(out=inv[i][:], in_=total[i])
+            if i < TILES - 1:
+                nc.scalar.activation(out=prob[i][:], in_=e[i][:], func=ACT.Copy, scale=inv[i][:])
+            else:
+                nc.vector.tensor_scalar(out=prob[i][:], in0=e[i][:], scalar1=inv[i][:], scalar2=None, op0=ALU.mult)
+            nc.sync.dma_start(out=out[i * P : (i + 1) * P, :], in_=prob[i][:])
+
+        nc.vector.memset(scale_table[:].bitcast(I32), 0)
+        load_h(0)
+        nc.sync.dma_start(offs_sb[:], offs)
+        for q in range(4):
+            nc.sync.dma_start(
+                out=scale_table[32 * q : 32 * q + 4, :].bitcast(I32), in_=x_scales[0, 4 * q : 4 * q + 4, :].bitcast(I32)
+            )
+        nc.sync.dma_start(out=word_table[:].bitcast(I32), in_=x_words[0].rearrange("p n t -> p (n t)").bitcast(I32))
+        load_h(1)
+        nc.sync.dma_start(hist_sb[:], hist)
+        nc.sync.dma_start(out=counts_first[:], in_=cnt[0:P, :])
+        nc.sync.dma_start(out=counts_rest[:], in_=cnt[P:, :].rearrange("(i p) r -> p i r", p=P))
+
+        dst, src = cast_views(0)
+        nc.vector.tensor_copy(out=dst, in_=src)
+        nc.vector.tensor_copy(out=x_bytes[:], in_=scale_table[:].indirect(offs_sb[:]))
+        quantize_h(0)
+        for lo in (0, HALF):
+            nc.vector.tensor_copy(
+                out=x_codes[:, lo : lo + HALF], in_=word_table[:].indirect(offs_sb[:, lo // 16 : (lo + HALF) // 16])
+            )
+            logits(0, lo, lo + HALF)
+        penalty(0)
+        dst, src = cast_views(1)
+        nc.vector.tensor_copy(out=dst, in_=src)
+        gather(0)
+        quantize_h(1)
+        for i in range(1, TILES):
+            logits(i, 0, S)
+            penalty(i)
+        for i in range(TILES):
+            scatter(i)
+            if i > 0:
+                finish(i - 1)
+            if i + 1 < TILES:
+                gather(i + 1)
+            row_max(i)
+        finish(TILES - 1)

@@ -45,12 +45,15 @@ def tile_picked_yrepp_pen_p_kernel(tc, x_words, x_scales, hT, cnt, offs, hist, o
         counts_first = keep.tile([P, R], F32, name="counts_first")
         counts_rest = keep.tile([P, TILES - 1, R], F32, name="counts_rest")
         counts = [counts_first[:]] + [counts_rest[:, i, :] for i in range(TILES - 1)]
-        drop = per_tile("drop", [P, R], F32)
-        z = per_tile("z", [P, S], F32)
-        slots = [keep.tile([P, R], F32, name="picked%d" % u) for u in range(2)]
-        picked = [slots[i % 2] for i in range(TILES)]
-        neg_max = per_tile("neg_max", [P, 1], F32)
-        total = [picked[i][:, 0:1] for i in range(TILES)]
+        drops = [keep.tile([P, R], F32, name="drop%d" % u) for u in range(2)]
+        drop = [drops[i % 2] for i in range(TILES)]
+        ring = [keep.tile([P, S + 8], F32, name="z%d" % u) for u in range(3)]
+        z = [ring[i % 3] for i in range(TILES)]
+        picked = per_tile("picked", [P, R], F32)
+        shift = keep.tile([P, 1], F32, name="shift")
+        neg_max = [shift] * TILES
+        sums = per_tile("sums", [P, 1], F32)
+        total = [z[2][:, S : S + 1], z[3][:, S : S + 1], sums[2][:], sums[3][:]]
         inv = per_tile("inv", [P, 1], F32)
         e = per_tile("e", [P, S], F32)
         prob = per_tile("prob", [P, S], F32)
@@ -89,22 +92,27 @@ def tile_picked_yrepp_pen_p_kernel(tc, x_words, x_scales, hT, cnt, offs, hist, o
             nc.scalar.activation(out=z[i][:, lo:hi], in_=acc[:], func=ACT.Copy)
 
         def gather(i):
-            nc.vector.tensor_copy(out=picked[i][:], in_=z[i][:].indirect(hist_sb[:]))
+            nc.vector.tensor_copy(out=picked[i][:], in_=z[i][:, 0:S].indirect(hist_sb[:]))
 
         def scatter(i):
             nc.vector.tensor_tensor(out=z[i][:].indirect(hist_sb[:]), in0=picked[i][:], in1=drop[i][:], op=ALU.add)
 
         def row_max(i):
-            nc.vector.tensor_reduce(out=neg_max[i][:], in_=z[i][:], axis=AXIS.X, op=ALU.max, negate=True)
-            nc.scalar.activation(out=e[i][:], in_=z[i][:], func=ACT.Exp, bias=neg_max[i][:], accum_out=total[i])
+            nc.vector.tensor_reduce(out=neg_max[i][:], in_=z[i][:, 0:S], axis=AXIS.X, op=ALU.max, negate=True)
+            nc.scalar.activation(out=e[i][:], in_=z[i][:, 0:S], func=ACT.Exp, bias=neg_max[i][:], accum_out=total[i])
 
         def finish(i):
             nc.vector.reciprocal(out=inv[i][:], in_=total[i])
             if i < TILES - 1:
                 nc.scalar.activation(out=prob[i][:], in_=e[i][:], func=ACT.Copy, scale=inv[i][:])
+                nc.sync.dma_start(out=out[i * P : (i + 1) * P, :], in_=prob[i][:])
             else:
-                nc.vector.tensor_scalar(out=prob[i][:], in0=e[i][:], scalar1=inv[i][:], scalar2=None, op0=ALU.mult)
-            nc.sync.dma_start(out=out[i * P : (i + 1) * P, :], in_=prob[i][:])
+                for lo, queue in ((0, nc.scalar), (HALF, nc.sync)):
+                    cols = slice(lo, lo + HALF)
+                    nc.vector.tensor_scalar(
+                        out=prob[i][:, cols], in0=e[i][:, cols], scalar1=inv[i][:], scalar2=None, op0=ALU.mult
+                    )
+                    queue.dma_start(out=out[i * P : (i + 1) * P, cols], in_=prob[i][:, cols])
 
         nc.vector.memset(scale_table[:].bitcast(I32), 0)
         load_h(0)
@@ -133,9 +141,9 @@ def tile_picked_yrepp_pen_p_kernel(tc, x_words, x_scales, hT, cnt, offs, hist, o
         nc.vector.tensor_copy(out=dst, in_=src)
         gather(0)
         quantize_h(1)
-        for i in range(1, TILES):
-            logits(i, 0, S)
-            penalty(i)
+        logits(1, 0, S)
+        penalty(1)
+        logits(2, 0, S)
         for i in range(TILES):
             scatter(i)
             if i > 0:
@@ -143,4 +151,8 @@ def tile_picked_yrepp_pen_p_kernel(tc, x_words, x_scales, hT, cnt, offs, hist, o
             if i + 1 < TILES:
                 gather(i + 1)
             row_max(i)
+            if i == 0:
+                logits(3, 0, S)
+            if i + 2 < TILES:
+                penalty(i + 2)
         finish(TILES - 1)

@@ -27,40 +27,50 @@ def tile_picked_yrepp_pen_p_kernel(tc, x_words, x_scales, hT, cnt, offs, hist, o
     with ExitStack() as ctx:
         keep = ctx.enter_context(tc.tile_pool(name="keep", bufs=1))
         psum = ctx.enter_context(tc.psum_pool(name="psum", bufs=1))
+        reuse = ctx.enter_context(tc.tile_pool(name="reuse", bufs=1))
 
         offs_sb = keep.tile([P, S // 16], U16, name="offs_sb")
         hist_sb = keep.tile([P, R // 16], U16, name="hist_sb")
         word_table = keep.tile([P, T], U32, name="word_table")
-        scale_table = keep.tile([P, T], U8, name="scale_table")
+        scale_table = reuse.tile([P, T], U8, name="scale_table", offset=2048)
+        picked_bytes = keep.tile([P, S], U8, name="picked_bytes")
         x_codes = keep.tile([P, S], U32, name="x_codes", align_bytes=64)
         x_bytes = keep.tile([P, S], U8, name="x_bytes", align_bytes=64)
 
         def per_tile(name, shape, dtype):
             return [keep.tile(shape, dtype, name="%s%d" % (name, i), align_bytes=64) for i in range(TILES)]
 
-        h_raw = [keep.tile([P, PACK, 2 * P], F32, name="h_raw%d" % u) for u in range(2)]
-        h_bf = [keep.tile([P, 2 * P, PACK], BF16, name="h_bf%d" % u, align_bytes=64) for u in range(2)]
-        h_codes = [keep.tile([P, 2 * P], U32, name="h_codes%d" % u, align_bytes=64) for u in range(2)]
-        h_bytes = [keep.tile([P, 2 * P], U8, name="h_bytes%d" % u, align_bytes=64) for u in range(2)]
-        counts_first = keep.tile([P, R], F32, name="counts_first")
-        counts_rest = keep.tile([P, TILES - 1, R], F32, name="counts_rest")
+        widths = (P, P, 2 * P)
+        starts = (0, P, 2 * P)
+        h_raw = [
+            reuse.tile([P, PACK, P], F32, name="h_raw0", offset=7200),
+            keep.tile([P, PACK, P], F32, name="h_raw1"),
+            reuse.tile([P, PACK, 2 * P], F32, name="h_raw2", offset=3104),
+        ]
+        h_bf = [keep.tile([P, widths[u], PACK], BF16, name="h_bf%d" % u, align_bytes=64) for u in range(3)]
+        h_codes = [keep.tile([P, widths[u]], U32, name="h_codes%d" % u, align_bytes=64) for u in range(2)]
+        h_codes.append(reuse.tile([P, widths[2]], U32, name="h_codes2", align_bytes=64, offset=10304))
+        h_bytes = [keep.tile([P, widths[u]], U8, name="h_bytes%d" % u, align_bytes=64) for u in range(3)]
+        counts_first = reuse.tile([P, R], F32, name="counts_first", offset=2080)
+        counts_rest = reuse.tile([P, TILES - 1, R], F32, name="counts_rest", offset=7200)
         counts = [counts_first[:]] + [counts_rest[:, i, :] for i in range(TILES - 1)]
-        drops = [keep.tile([P, R], F32, name="drop%d" % u) for u in range(2)]
+        drops = [keep.tile([P, R], F32, name="drop0"), reuse.tile([P, R], F32, name="drop1", offset=4096)]
         drop = [drops[i % 2] for i in range(TILES)]
         ring = [keep.tile([P, S + 8], F32, name="z%d" % u) for u in range(3)]
         z = [ring[i % 3] for i in range(TILES)]
         picked = per_tile("picked", [P, R], F32)
-        shift = keep.tile([P, 1], F32, name="shift")
+        shift = reuse.tile([P, 1], F32, name="shift", offset=5120)
         neg_max = [shift] * TILES
         sums = per_tile("sums", [P, 1], F32)
         total = [z[2][:, S : S + 1], z[3][:, S : S + 1], sums[2][:], sums[3][:]]
         inv = per_tile("inv", [P, 1], F32)
-        e = per_tile("e", [P, S], F32)
+        e = [reuse.tile([P, S], F32, name="e0", offset=10304)]
+        e.extend(keep.tile([P, S], F32, name="e%d" % i) for i in range(1, TILES))
         prob = per_tile("prob", [P, S], F32)
 
         def load_h(u):
             nc.sync.dma_start(
-                out=h_raw[u][:], in_=hT[:, 2 * u * P : 2 * (u + 1) * P].rearrange("(p j) w -> p j w", j=PACK)
+                out=h_raw[u][:], in_=hT[:, starts[u] : starts[u] + widths[u]].rearrange("(p j) w -> p j w", j=PACK)
             )
 
         def cast_views(u):
@@ -77,19 +87,26 @@ def tile_picked_yrepp_pen_p_kernel(tc, x_words, x_scales, hT, cnt, offs, hist, o
         def penalty(i):
             nc.scalar.activation(out=drop[i][:], in_=counts[i], func=ACT.Copy, scale=-0.3, bias=-0.2)
 
-        def logits(i, lo, hi):
-            cols = slice((i % 2) * P, (i % 2 + 1) * P)
+        def product(i, lo, hi):
+            u = min(i, 2)
+            cols = slice(i * P - starts[u], (i + 1) * P - starts[u])
             acc = psum.tile([P, hi - lo], F32, name="acc%d_%d" % (i, lo))
             nc.tensor.matmul_mx(
                 out=acc[:],
-                lhsT=h_codes[i // 2][:, cols].bitcast(FP8X4),
-                lhsT_scale=h_bytes[i // 2][:, cols],
+                lhsT=h_codes[u][:, cols].bitcast(FP8X4),
+                lhsT_scale=h_bytes[u][:, cols],
                 rhs=x_codes[:, lo:hi].bitcast(FP8X4),
                 rhs_scale=x_bytes[:, lo:hi],
                 start=True,
                 stop=True,
             )
+            return acc
+
+        def empty(i, lo, hi, acc):
             nc.scalar.activation(out=z[i][:, lo:hi], in_=acc[:], func=ACT.Copy)
+
+        def logits(i, lo, hi):
+            empty(i, lo, hi, product(i, lo, hi))
 
         def gather(i):
             nc.vector.tensor_copy(out=picked[i][:], in_=z[i][:, 0:S].indirect(hist_sb[:]))
@@ -114,45 +131,56 @@ def tile_picked_yrepp_pen_p_kernel(tc, x_words, x_scales, hT, cnt, offs, hist, o
                     )
                     queue.dma_start(out=out[i * P : (i + 1) * P, cols], in_=prob[i][:, cols])
 
-        nc.vector.memset(scale_table[:].bitcast(I32), 0)
-        load_h(0)
+        nc.scalar.dma_start(out=scale_table[16:32, :].bitcast(I32), in_=x_scales[0].bitcast(I32))
         nc.sync.dma_start(offs_sb[:], offs)
-        for q in range(4):
-            nc.sync.dma_start(
-                out=scale_table[32 * q : 32 * q + 4, :].bitcast(I32), in_=x_scales[0, 4 * q : 4 * q + 4, :].bitcast(I32)
-            )
+        load_h(0)
+        nc.sync.dma_start(hist_sb[:], hist)
         nc.sync.dma_start(out=word_table[:].bitcast(I32), in_=x_words[0].rearrange("p n t -> p (n t)").bitcast(I32))
         load_h(1)
-        nc.sync.dma_start(hist_sb[:], hist)
+        for lo, hi in ((0, 16), (32, 64), (64, P)):
+            nc.vector.memset(scale_table[lo:hi, :].bitcast(I32), 0)
+        nc.vector.memset(x_bytes[:].bitcast(I32), 0)
+
+        nc.vector.tensor_copy(out=picked_bytes[:], in_=scale_table[:].indirect(offs_sb[:]))
+        for q in range(4):
+            (nc.sync, nc.scalar)[q % 2].dma_start(
+                out=x_bytes[32 * q : 32 * q + 4, :].bitcast(I32),
+                in_=picked_bytes[16 + 4 * q : 20 + 4 * q, :].bitcast(I32),
+            )
         nc.sync.dma_start(out=counts_first[:], in_=cnt[0:P, :])
-        nc.sync.dma_start(out=counts_rest[:], in_=cnt[P:, :].rearrange("(i p) r -> p i r", p=P))
+        load_h(2)
 
         dst, src = cast_views(0)
         nc.vector.tensor_copy(out=dst, in_=src)
-        nc.vector.tensor_copy(out=x_bytes[:], in_=scale_table[:].indirect(offs_sb[:]))
+        nc.sync.dma_start(out=counts_rest[:], in_=cnt[P:, :].rearrange("(i p) r -> p i r", p=P))
         quantize_h(0)
         for lo in (0, HALF):
             nc.vector.tensor_copy(
                 out=x_codes[:, lo : lo + HALF], in_=word_table[:].indirect(offs_sb[:, lo // 16 : (lo + HALF) // 16])
             )
             logits(0, lo, lo + HALF)
-        penalty(0)
         dst, src = cast_views(1)
         nc.vector.tensor_copy(out=dst, in_=src)
-        gather(0)
         quantize_h(1)
+        penalty(0)
+        gather(0)
         logits(1, 0, S)
+        dst, src = cast_views(2)
+        nc.scalar.activation(out=dst, in_=src, func=ACT.Copy)
         penalty(1)
-        logits(2, 0, S)
         for i in range(TILES):
             scatter(i)
             if i > 0:
                 finish(i - 1)
             if i + 1 < TILES:
                 gather(i + 1)
+            if i == 0:
+                quantize_h(2)
+                acc = [product(2, 0, S), product(3, 0, S)]
+                empty(2, 0, S, acc[0])
             row_max(i)
             if i == 0:
-                logits(3, 0, S)
+                empty(3, 0, S, acc[1])
             if i + 2 < TILES:
                 penalty(i + 2)
         finish(TILES - 1)

@@ -32,7 +32,7 @@ def tile_picked_yrepp_pen_p_kernel(tc, x_words, x_scales, hT, cnt, offs, hist, o
         offs_sb = keep.tile([P, S // 16], U16, name="offs_sb")
         hist_sb = keep.tile([P, R // 16], U16, name="hist_sb")
         word_table = keep.tile([P, T], U32, name="word_table")
-        scale_table = reuse.tile([P, T], U8, name="scale_table", offset=2048)
+        scale_table = keep.tile([P, T], U8, name="scale_table")
         picked_bytes = keep.tile([P, S], U8, name="picked_bytes")
         x_codes = keep.tile([P, S], U32, name="x_codes", align_bytes=64)
         x_bytes = keep.tile([P, S], U8, name="x_bytes", align_bytes=64)
@@ -43,28 +43,29 @@ def tile_picked_yrepp_pen_p_kernel(tc, x_words, x_scales, hT, cnt, offs, hist, o
         widths = (P, P, 2 * P)
         starts = (0, P, 2 * P)
         h_raw = [
-            reuse.tile([P, PACK, P], F32, name="h_raw0", offset=7200),
-            keep.tile([P, PACK, P], F32, name="h_raw1"),
-            reuse.tile([P, PACK, 2 * P], F32, name="h_raw2", offset=3104),
+            keep.tile([P, PACK, P], F32, name="h_raw0"),
+            reuse.tile([P, PACK, P], F32, name="h_raw1", offset=5120),
+            reuse.tile([P, PACK, 2 * P], F32, name="h_raw2", offset=1024),
         ]
-        h_bf = [keep.tile([P, widths[u], PACK], BF16, name="h_bf%d" % u, align_bytes=64) for u in range(3)]
-        h_codes = [keep.tile([P, widths[u]], U32, name="h_codes%d" % u, align_bytes=64) for u in range(2)]
-        h_codes.append(reuse.tile([P, widths[2]], U32, name="h_codes2", align_bytes=64, offset=10304))
+        h_bf = [reuse.tile([P, P, PACK], BF16, name="h_bf0", align_bytes=64, offset=960)]
+        h_bf.extend(keep.tile([P, widths[u], PACK], BF16, name="h_bf%d" % u, align_bytes=64) for u in (1, 2))
+        h_codes = [reuse.tile([P, P], U32, name="h_codes%d" % u, align_bytes=64, offset=10240) for u in range(2)]
+        h_codes.append(reuse.tile([P, widths[2]], U32, name="h_codes2", align_bytes=64, offset=8192))
         h_bytes = [keep.tile([P, widths[u]], U8, name="h_bytes%d" % u, align_bytes=64) for u in range(3)]
-        counts_first = reuse.tile([P, R], F32, name="counts_first", offset=2080)
-        counts_rest = reuse.tile([P, TILES - 1, R], F32, name="counts_rest", offset=7200)
+        counts_first = reuse.tile([P, R], F32, name="counts_first", offset=0)
+        counts_rest = reuse.tile([P, TILES - 1, R], F32, name="counts_rest", offset=5120)
         counts = [counts_first[:]] + [counts_rest[:, i, :] for i in range(TILES - 1)]
-        drops = [keep.tile([P, R], F32, name="drop0"), reuse.tile([P, R], F32, name="drop1", offset=4096)]
+        drops = [keep.tile([P, R], F32, name="drop0"), reuse.tile([P, R], F32, name="drop1", offset=2048)]
         drop = [drops[i % 2] for i in range(TILES)]
         ring = [keep.tile([P, S + 8], F32, name="z%d" % u) for u in range(3)]
         z = [ring[i % 3] for i in range(TILES)]
         picked = per_tile("picked", [P, R], F32)
-        shift = reuse.tile([P, 1], F32, name="shift", offset=5120)
+        shift = reuse.tile([P, 1], F32, name="shift", offset=4096)
         neg_max = [shift] * TILES
         sums = per_tile("sums", [P, 1], F32)
         total = [z[2][:, S : S + 1], z[3][:, S : S + 1], sums[2][:], sums[3][:]]
         inv = per_tile("inv", [P, 1], F32)
-        e = [reuse.tile([P, S], F32, name="e0", offset=10304)]
+        e = [reuse.tile([P, S], F32, name="e0", offset=8192)]
         e.extend(keep.tile([P, S], F32, name="e%d" % i) for i in range(1, TILES))
         prob = per_tile("prob", [P, S], F32)
 
@@ -143,24 +144,28 @@ def tile_picked_yrepp_pen_p_kernel(tc, x_words, x_scales, hT, cnt, offs, hist, o
 
         nc.vector.tensor_copy(out=picked_bytes[:], in_=scale_table[:].indirect(offs_sb[:]))
         for q in range(4):
-            (nc.sync, nc.scalar)[q % 2].dma_start(
+            nc.scalar.dma_start(
                 out=x_bytes[32 * q : 32 * q + 4, :].bitcast(I32),
                 in_=picked_bytes[16 + 4 * q : 20 + 4 * q, :].bitcast(I32),
             )
-        nc.sync.dma_start(out=counts_first[:], in_=cnt[0:P, :])
-        load_h(2)
 
         dst, src = cast_views(0)
         nc.vector.tensor_copy(out=dst, in_=src)
-        nc.sync.dma_start(out=counts_rest[:], in_=cnt[P:, :].rearrange("(i p) r -> p i r", p=P))
         quantize_h(0)
+        nc.sync.dma_start(out=counts_first[:], in_=cnt[0:P, :])
+        load_h(2)
         for lo in (0, HALF):
             nc.vector.tensor_copy(
                 out=x_codes[:, lo : lo + HALF], in_=word_table[:].indirect(offs_sb[:, lo // 16 : (lo + HALF) // 16])
             )
-            logits(0, lo, lo + HALF)
+            if lo == 0:
+                logits(0, lo, lo + HALF)
+        logits(0, HALF, HALF + P)
+        last = product(0, HALF + P, S)
         dst, src = cast_views(1)
         nc.vector.tensor_copy(out=dst, in_=src)
+        nc.sync.dma_start(out=counts_rest[:], in_=cnt[P:, :].rearrange("(i p) r -> p i r", p=P))
+        nc.vector.tensor_copy(out=z[0][:, HALF + P : S], in_=last[:])
         quantize_h(1)
         penalty(0)
         gather(0)

@@ -125,12 +125,13 @@ def tile_picked_yrepp_pen_p_kernel(tc, x_words, x_scales, hT, cnt, offs, hist, o
                 nc.scalar.activation(out=prob[i][:], in_=e[i][:], func=ACT.Copy, scale=inv[i][:])
                 nc.sync.dma_start(out=out[i * P : (i + 1) * P, :], in_=prob[i][:])
             else:
-                for lo, queue in ((0, nc.scalar), (HALF, nc.sync)):
-                    cols = slice(lo, lo + HALF)
-                    nc.vector.tensor_scalar(
-                        out=prob[i][:, cols], in0=e[i][:, cols], scalar1=inv[i][:], scalar2=None, op0=ALU.mult
-                    )
-                    queue.dma_start(out=out[i * P : (i + 1) * P, cols], in_=prob[i][:, cols])
+                rows = slice(i * P, (i + 1) * P)
+                nc.scalar.activation(out=prob[i][:, :HALF], in_=e[i][:, :HALF], func=ACT.Copy, scale=inv[i][:])
+                nc.scalar.dma_start(out=out[rows, :HALF], in_=prob[i][:, :HALF])
+                nc.vector.tensor_scalar(
+                    out=prob[i][:, HALF:], in0=e[i][:, HALF:], scalar1=inv[i][:], scalar2=None, op0=ALU.mult
+                )
+                nc.sync.dma_start(out=out[rows, HALF:], in_=prob[i][:, HALF:])
 
         nc.scalar.dma_start(out=scale_table[16:32, :].bitcast(I32), in_=x_scales[0].bitcast(I32))
         nc.sync.dma_start(offs_sb[:], offs)

@@ -49,7 +49,7 @@ def tile_picked_yrepp_pen_p_kernel(tc, x_words, x_scales, hT, cnt, offs, hist, o
         ]
         h_bf = [reuse.tile([P, P, PACK], BF16, name="h_bf0", align_bytes=64, offset=960)]
         h_bf.extend(keep.tile([P, widths[u], PACK], BF16, name="h_bf%d" % u, align_bytes=64) for u in (1, 2))
-        h_codes = [reuse.tile([P, P], U32, name="h_codes%d" % u, align_bytes=64, offset=10240) for u in range(2)]
+        h_codes = [keep.tile([P, P], U32, name="h_codes%d" % u, align_bytes=64) for u in range(2)]
         h_codes.append(reuse.tile([P, widths[2]], U32, name="h_codes2", align_bytes=64, offset=8192))
         h_bytes = [keep.tile([P, widths[u]], U8, name="h_bytes%d" % u, align_bytes=64) for u in range(3)]
         counts_first = reuse.tile([P, R], F32, name="counts_first", offset=0)
@@ -145,13 +145,13 @@ def tile_picked_yrepp_pen_p_kernel(tc, x_words, x_scales, hT, cnt, offs, hist, o
 
         nc.vector.tensor_copy(out=picked_bytes[:], in_=scale_table[:].indirect(offs_sb[:]))
         for q in range(4):
-            nc.scalar.dma_start(
+            nc.sync.dma_start(
                 out=x_bytes[32 * q : 32 * q + 4, :].bitcast(I32),
                 in_=picked_bytes[16 + 4 * q : 20 + 4 * q, :].bitcast(I32),
             )
 
         dst, src = cast_views(0)
-        nc.vector.tensor_copy(out=dst, in_=src)
+        nc.scalar.activation(out=dst, in_=src, func=ACT.Copy)
         quantize_h(0)
         nc.sync.dma_start(out=counts_first[:], in_=cnt[0:P, :])
         load_h(2)
@@ -160,13 +160,13 @@ def tile_picked_yrepp_pen_p_kernel(tc, x_words, x_scales, hT, cnt, offs, hist, o
                 out=x_codes[:, lo : lo + HALF], in_=word_table[:].indirect(offs_sb[:, lo // 16 : (lo + HALF) // 16])
             )
             if lo == 0:
-                logits(0, lo, lo + HALF)
-        logits(0, HALF, HALF + P)
-        last = product(0, HALF + P, S)
+                first = product(0, 0, HALF)
         dst, src = cast_views(1)
-        nc.vector.tensor_copy(out=dst, in_=src)
+        nc.scalar.activation(out=dst, in_=src, func=ACT.Copy)
+        logits(0, HALF, HALF + P)
+        logits(0, HALF + P, S)
         nc.sync.dma_start(out=counts_rest[:], in_=cnt[P:, :].rearrange("(i p) r -> p i r", p=P))
-        nc.vector.tensor_copy(out=z[0][:, HALF + P : S], in_=last[:])
+        nc.vector.tensor_copy(out=z[0][:, :HALF], in_=first[:])
         quantize_h(1)
         penalty(0)
         gather(0)

@@ -20,6 +20,7 @@ P = 128
 PACK = 4
 TILES = V // P
 HALF = S // 2
+SPLIT = 3 * R // 4
 
 
 def tile_picked_yrepp_pen_p_kernel(tc, x_words, x_scales, hT, cnt, offs, hist, out):
@@ -33,51 +34,53 @@ def tile_picked_yrepp_pen_p_kernel(tc, x_words, x_scales, hT, cnt, offs, hist, o
         hist_sb = keep.tile([P, R // 16], U16, name="hist_sb")
         word_table = keep.tile([P, T], U32, name="word_table")
         scale_table = keep.tile([P, T], U8, name="scale_table")
-        picked_bytes = keep.tile([P, S], U8, name="picked_bytes")
+        picked_bytes = reuse.tile([P, S], U8, name="picked_bytes", offset=17408)
         x_codes = keep.tile([P, S], U32, name="x_codes", align_bytes=64)
         x_bytes = keep.tile([P, S], U8, name="x_bytes", align_bytes=64)
 
         def per_tile(name, shape, dtype):
             return [keep.tile(shape, dtype, name="%s%d" % (name, i), align_bytes=64) for i in range(TILES)]
 
-        widths = (P, P, 2 * P)
-        starts = (0, P, 2 * P)
         h_raw = [
-            keep.tile([P, PACK, P], F32, name="h_raw0"),
-            reuse.tile([P, PACK, P], F32, name="h_raw1", offset=5120),
-            reuse.tile([P, PACK, 2 * P], F32, name="h_raw2", offset=1024),
+            reuse.tile([P, PACK, P], F32, name="h_raw%d" % u, offset=at) for u, at in enumerate((0, 6144, 4000, 6144))
         ]
-        h_bf = [reuse.tile([P, P, PACK], BF16, name="h_bf0", align_bytes=64, offset=960)]
-        h_bf.extend(keep.tile([P, widths[u], PACK], BF16, name="h_bf%d" % u, align_bytes=64) for u in (1, 2))
-        h_codes = [keep.tile([P, P], U32, name="h_codes%d" % u, align_bytes=64) for u in range(2)]
-        h_codes.append(reuse.tile([P, widths[2]], U32, name="h_codes2", align_bytes=64, offset=8192))
-        h_bytes = [keep.tile([P, widths[u]], U8, name="h_bytes%d" % u, align_bytes=64) for u in range(3)]
-        counts_first = reuse.tile([P, R], F32, name="counts_first", offset=0)
-        counts_rest = reuse.tile([P, TILES - 1, R], F32, name="counts_rest", offset=5120)
-        counts = [counts_first[:]] + [counts_rest[:, i, :] for i in range(TILES - 1)]
-        drops = [keep.tile([P, R], F32, name="drop0"), reuse.tile([P, R], F32, name="drop1", offset=2048)]
+        h_bf = [
+            reuse.tile([P, P, PACK], BF16, name="h_bf%d" % u, align_bytes=64, offset=at)
+            for u, at in enumerate((3008, 12288, 14400, 14400))
+        ]
+        h_codes = [reuse.tile([P, P], U32, name="h_codes0", align_bytes=64, offset=15360)]
+        h_codes.extend(keep.tile([P, P], U32, name="h_codes%d" % u, align_bytes=64) for u in (1, 2))
+        h_codes.append(reuse.tile([P, P], U32, name="h_codes3", align_bytes=64, offset=9216))
+        h_bytes = [keep.tile([P, P], U8, name="h_bytes%d" % u, align_bytes=64) for u in range(TILES)]
+        counts_first = reuse.tile([P, R], F32, name="counts_first", offset=2048)
+        counts_second = reuse.tile([P, R], F32, name="counts_second", offset=17408)
+        counts_rest = reuse.tile([P, TILES - 2, R], F32, name="counts_rest", offset=4000)
+        counts = [counts_first[:], counts_second[:]] + [counts_rest[:, i, :] for i in range(TILES - 2)]
+        drops = [reuse.tile([P, R], F32, name="drop0", offset=15808), reuse.tile([P, R], F32, name="drop1", offset=6144)]
         drop = [drops[i % 2] for i in range(TILES)]
-        ring = [keep.tile([P, S + 8], F32, name="z%d" % u) for u in range(3)]
+        ring = [keep.tile([P, S + 8], F32, name="z%d" % u) for u in range(2)]
+        ring.append(reuse.tile([P, S + 8], F32, name="z2", offset=13312))
         z = [ring[i % 3] for i in range(TILES)]
         picked = per_tile("picked", [P, R], F32)
-        shift = reuse.tile([P, 1], F32, name="shift", offset=4096)
+        shift = reuse.tile([P, 1], F32, name="shift", offset=7168)
         neg_max = [shift] * TILES
         sums = per_tile("sums", [P, 1], F32)
         total = [z[2][:, S : S + 1], z[3][:, S : S + 1], sums[2][:], sums[3][:]]
         inv = per_tile("inv", [P, 1], F32)
-        e = [reuse.tile([P, S], F32, name="e0", offset=8192)]
+        e = [reuse.tile([P, S], F32, name="e0", offset=10240)]
         e.extend(keep.tile([P, S], F32, name="e%d" % i) for i in range(1, TILES))
         prob = per_tile("prob", [P, S], F32)
 
         def load_h(u):
             nc.sync.dma_start(
-                out=h_raw[u][:], in_=hT[:, starts[u] : starts[u] + widths[u]].rearrange("(p j) w -> p j w", j=PACK)
+                out=h_raw[u][:], in_=hT[:, u * P : (u + 1) * P].rearrange("(p j) w -> p j w", j=PACK)
             )
 
-        def cast_views(u):
-            return (
-                h_bf[u][:].rearrange("p (c w) j -> p c j w", w=4),
-                h_raw[u][:].rearrange("p j (c w) -> p c j w", w=4),
+        def cast(u):
+            nc.scalar.activation(
+                out=h_bf[u][:].rearrange("p (c w) j -> p c j w", w=4),
+                in_=h_raw[u][:].rearrange("p j (c w) -> p c j w", w=4),
+                func=ACT.Copy,
             )
 
         def quantize_h(u):
@@ -89,13 +92,11 @@ def tile_picked_yrepp_pen_p_kernel(tc, x_words, x_scales, hT, cnt, offs, hist, o
             nc.scalar.activation(out=drop[i][:], in_=counts[i], func=ACT.Copy, scale=-0.3, bias=-0.2)
 
         def product(i, lo, hi):
-            u = min(i, 2)
-            cols = slice(i * P - starts[u], (i + 1) * P - starts[u])
             acc = psum.tile([P, hi - lo], F32, name="acc%d_%d" % (i, lo))
             nc.tensor.matmul_mx(
                 out=acc[:],
-                lhsT=h_codes[u][:, cols].bitcast(FP8X4),
-                lhsT_scale=h_bytes[u][:, cols],
+                lhsT=h_codes[i][:].bitcast(FP8X4),
+                lhsT_scale=h_bytes[i][:],
                 rhs=x_codes[:, lo:hi].bitcast(FP8X4),
                 rhs_scale=x_bytes[:, lo:hi],
                 start=True,
@@ -150,29 +151,34 @@ def tile_picked_yrepp_pen_p_kernel(tc, x_words, x_scales, hT, cnt, offs, hist, o
                 in_=picked_bytes[16 + 4 * q : 20 + 4 * q, :].bitcast(I32),
             )
 
-        dst, src = cast_views(0)
-        nc.scalar.activation(out=dst, in_=src, func=ACT.Copy)
+        cast(0)
         quantize_h(0)
-        nc.sync.dma_start(out=counts_first[:], in_=cnt[0:P, :])
         load_h(2)
+        nc.sync.dma_start(out=counts_first[:], in_=cnt[0:P, :])
         for lo in (0, HALF):
             nc.vector.tensor_copy(
                 out=x_codes[:, lo : lo + HALF], in_=word_table[:].indirect(offs_sb[:, lo // 16 : (lo + HALF) // 16])
             )
             if lo == 0:
-                first = product(0, 0, HALF)
-        dst, src = cast_views(1)
-        nc.scalar.activation(out=dst, in_=src, func=ACT.Copy)
+                logits(0, 0, HALF)
+        nc.vector.tensor_copy(
+            out=h_bf[1][:].rearrange("p (c w) j -> p c j w", w=4), in_=h_raw[1][:].rearrange("p j (c w) -> p c j w", w=4)
+        )
         logits(0, HALF, HALF + P)
         logits(0, HALF + P, S)
-        nc.sync.dma_start(out=counts_rest[:], in_=cnt[P:, :].rearrange("(i p) r -> p i r", p=P))
-        nc.vector.tensor_copy(out=z[0][:, :HALF], in_=first[:])
+        load_h(3)
+        nc.sync.dma_start(out=counts_second[:], in_=cnt[P : 2 * P, :])
         quantize_h(1)
-        penalty(0)
+        nc.vector.tensor_scalar(
+            out=drop[0][:, :SPLIT], in0=counts[0][:, :SPLIT], scalar1=-0.3, scalar2=-0.2, op0=ALU.mult, op1=ALU.add
+        )
+        cast(2)
+        nc.scalar.activation(out=drop[0][:, SPLIT:], in_=counts[0][:, SPLIT:], func=ACT.Copy, scale=-0.3, bias=-0.2)
+        nc.sync.dma_start(out=counts_rest[:], in_=cnt[2 * P :, :].rearrange("(i p) r -> p i r", p=P))
         gather(0)
+        quantize_h(2)
         logits(1, 0, S)
-        dst, src = cast_views(2)
-        nc.scalar.activation(out=dst, in_=src, func=ACT.Copy)
+        cast(3)
         penalty(1)
         for i in range(TILES):
             scatter(i)
@@ -181,7 +187,7 @@ def tile_picked_yrepp_pen_p_kernel(tc, x_words, x_scales, hT, cnt, offs, hist, o
             if i + 1 < TILES:
                 gather(i + 1)
             if i == 0:
-                quantize_h(2)
+                quantize_h(3)
                 acc = [product(2, 0, S), product(3, 0, S)]
                 empty(2, 0, S, acc[0])
             row_max(i)

@@ -33,7 +33,7 @@ def tile_picked_yrepp_pen_p_kernel(tc, x_words, x_scales, hT, cnt, offs, hist, o
         offs_sb = keep.tile([P, S // 16], U16, name="offs_sb")
         hist_sb = keep.tile([P, R // 16], U16, name="hist_sb")
         word_table = keep.tile([P, T], U32, name="word_table")
-        scale_table = keep.tile([P, T], U8, name="scale_table")
+        scale_table = reuse.tile([P, T], U8, name="scale_table", offset=21472)
         picked_bytes = reuse.tile([P, S], U8, name="picked_bytes", offset=17408)
         x_codes = keep.tile([P, S], U32, name="x_codes", align_bytes=64)
         x_bytes = keep.tile([P, S], U8, name="x_bytes", align_bytes=64)
@@ -42,7 +42,7 @@ def tile_picked_yrepp_pen_p_kernel(tc, x_words, x_scales, hT, cnt, offs, hist, o
             return [keep.tile(shape, dtype, name="%s%d" % (name, i), align_bytes=64) for i in range(TILES)]
 
         h_raw = [
-            reuse.tile([P, PACK, P], F32, name="h_raw%d" % u, offset=at) for u, at in enumerate((0, 6144, 4000, 6144))
+            reuse.tile([P, PACK, P], F32, name="h_raw%d" % u, offset=at) for u, at in enumerate((0, 21472, 4000, 23488))
         ]
         h_bf = [
             reuse.tile([P, P, PACK], BF16, name="h_bf%d" % u, align_bytes=64, offset=at)
@@ -56,13 +56,14 @@ def tile_picked_yrepp_pen_p_kernel(tc, x_words, x_scales, hT, cnt, offs, hist, o
         counts_second = reuse.tile([P, R], F32, name="counts_second", offset=17408)
         counts_rest = reuse.tile([P, TILES - 2, R], F32, name="counts_rest", offset=4000)
         counts = [counts_first[:], counts_second[:]] + [counts_rest[:, i, :] for i in range(TILES - 2)]
-        drops = [reuse.tile([P, R], F32, name="drop0", offset=15808), reuse.tile([P, R], F32, name="drop1", offset=6144)]
+        drops = [reuse.tile([P, R], F32, name="drop0", offset=15808), reuse.tile([P, R], F32, name="drop1", offset=23552)]
         drop = [drops[i % 2] for i in range(TILES)]
-        ring = [keep.tile([P, S + 8], F32, name="z%d" % u) for u in range(2)]
+        ring = [keep.tile([P, S + 8], F32, name="z0"), reuse.tile([P, S + 8], F32, name="z1", offset=960)]
         ring.append(reuse.tile([P, S + 8], F32, name="z2", offset=13312))
         z = [ring[i % 3] for i in range(TILES)]
-        picked = per_tile("picked", [P, R], F32)
-        shift = reuse.tile([P, 1], F32, name="shift", offset=7168)
+        picked = [reuse.tile([P, R], F32, name="picked0", offset=20480)]
+        picked.extend(keep.tile([P, R], F32, name="picked%d" % i) for i in range(1, TILES))
+        shift = reuse.tile([P, 1], F32, name="shift", offset=24576)
         neg_max = [shift] * TILES
         sums = per_tile("sums", [P, 1], F32)
         total = [z[2][:, S : S + 1], z[3][:, S : S + 1], sums[2][:], sums[3][:]]
@@ -139,7 +140,6 @@ def tile_picked_yrepp_pen_p_kernel(tc, x_words, x_scales, hT, cnt, offs, hist, o
         load_h(0)
         nc.sync.dma_start(hist_sb[:], hist)
         nc.sync.dma_start(out=word_table[:].bitcast(I32), in_=x_words[0].rearrange("p n t -> p (n t)").bitcast(I32))
-        load_h(1)
         for lo, hi in ((0, 16), (32, 64), (64, P)):
             nc.vector.memset(scale_table[lo:hi, :].bitcast(I32), 0)
         nc.vector.memset(x_bytes[:].bitcast(I32), 0)
@@ -150,6 +150,7 @@ def tile_picked_yrepp_pen_p_kernel(tc, x_words, x_scales, hT, cnt, offs, hist, o
                 out=x_bytes[32 * q : 32 * q + 4, :].bitcast(I32),
                 in_=picked_bytes[16 + 4 * q : 20 + 4 * q, :].bitcast(I32),
             )
+        load_h(1)
 
         cast(0)
         quantize_h(0)

@@ -129,17 +129,16 @@ def tile_picked_yrepp_pen_p_kernel(tc, x_words, x_scales, hT, cnt, offs, hist, o
             else:
                 rows = slice(i * P, (i + 1) * P)
                 nc.scalar.activation(out=prob[i][:, :HALF], in_=e[i][:, :HALF], func=ACT.Copy, scale=inv[i][:])
-                nc.scalar.dma_start(out=out[rows, :HALF], in_=prob[i][:, :HALF])
                 nc.vector.tensor_scalar(
                     out=prob[i][:, HALF:], in0=e[i][:, HALF:], scalar1=inv[i][:], scalar2=None, op0=ALU.mult
                 )
-                nc.sync.dma_start(out=out[rows, HALF:], in_=prob[i][:, HALF:])
+                nc.sync.dma_start(out=out[rows, :], in_=prob[i][:])
 
         nc.scalar.dma_start(out=scale_table[16:32, :].bitcast(I32), in_=x_scales[0].bitcast(I32))
         nc.sync.dma_start(offs_sb[:], offs)
         load_h(0)
-        nc.sync.dma_start(hist_sb[:], hist)
         nc.sync.dma_start(out=word_table[:].bitcast(I32), in_=x_words[0].rearrange("p n t -> p (n t)").bitcast(I32))
+        nc.sync.dma_start(hist_sb[:], hist)
         for lo, hi in ((0, 16), (32, 64), (64, P)):
             nc.vector.memset(scale_table[lo:hi, :].bitcast(I32), 0)
         nc.vector.memset(x_bytes[:].bitcast(I32), 0)

@@ -20,7 +20,6 @@ P = 128
 PACK = 4
 TILES = V // P
 HALF = S // 2
-SPLIT = 3 * R // 4
 
 
 def tile_picked_yrepp_pen_p_kernel(tc, x_words, x_scales, hT, cnt, offs, hist, out):
@@ -30,58 +29,48 @@ def tile_picked_yrepp_pen_p_kernel(tc, x_words, x_scales, hT, cnt, offs, hist, o
         psum = ctx.enter_context(tc.psum_pool(name="psum", bufs=1))
         reuse = ctx.enter_context(tc.tile_pool(name="reuse", bufs=1))
 
+        def placed(name, shape, dtype, places, **kw):
+            return [
+                keep.tile(shape, dtype, name="%s%d" % (name, i), **kw)
+                if at is None
+                else reuse.tile(shape, dtype, name="%s%d" % (name, i), offset=at, **kw)
+                for i, at in enumerate(places)
+            ]
+
         offs_sb = keep.tile([P, S // 16], U16, name="offs_sb")
         hist_sb = keep.tile([P, R // 16], U16, name="hist_sb")
         word_table = keep.tile([P, T], U32, name="word_table")
-        scale_table = reuse.tile([P, T], U8, name="scale_table", offset=21472)
-        picked_bytes = reuse.tile([P, S], U8, name="picked_bytes", offset=17408)
+        scale_table = reuse.tile([P, T], U8, name="scale_table", offset=2016)
+        picked_bytes = reuse.tile([P, S], U8, name="picked_bytes", offset=25536)
         x_codes = keep.tile([P, S], U32, name="x_codes", align_bytes=64)
         x_bytes = keep.tile([P, S], U8, name="x_bytes", align_bytes=64)
 
-        def per_tile(name, shape, dtype):
-            return [keep.tile(shape, dtype, name="%s%d" % (name, i), align_bytes=64) for i in range(TILES)]
-
-        h_raw = [
-            reuse.tile([P, PACK, P], F32, name="h_raw%d" % u, offset=at) for u, at in enumerate((0, 21472, 4000, 23488))
-        ]
-        h_bf = [
-            reuse.tile([P, P, PACK], BF16, name="h_bf%d" % u, align_bytes=64, offset=at)
-            for u, at in enumerate((3008, 12288, 14400, 14400))
-        ]
-        h_codes = [reuse.tile([P, P], U32, name="h_codes0", align_bytes=64, offset=15360)]
-        h_codes.extend(keep.tile([P, P], U32, name="h_codes%d" % u, align_bytes=64) for u in (1, 2))
-        h_codes.append(reuse.tile([P, P], U32, name="h_codes3", align_bytes=64, offset=9216))
-        h_bytes = [keep.tile([P, P], U8, name="h_bytes%d" % u, align_bytes=64) for u in range(TILES)]
-        counts_first = reuse.tile([P, R], F32, name="counts_first", offset=2048)
-        counts_second = reuse.tile([P, R], F32, name="counts_second", offset=17408)
-        counts_rest = reuse.tile([P, TILES - 2, R], F32, name="counts_rest", offset=4000)
-        counts = [counts_first[:], counts_second[:]] + [counts_rest[:, i, :] for i in range(TILES - 2)]
-        drops = [reuse.tile([P, R], F32, name="drop0", offset=15808), reuse.tile([P, R], F32, name="drop1", offset=23552)]
-        drop = [drops[i % 2] for i in range(TILES)]
-        ring = [keep.tile([P, S + 8], F32, name="z0"), reuse.tile([P, S + 8], F32, name="z1", offset=960)]
-        ring.append(reuse.tile([P, S + 8], F32, name="z2", offset=13312))
-        z = [ring[i % 3] for i in range(TILES)]
-        picked = [reuse.tile([P, R], F32, name="picked0", offset=20480)]
-        picked.extend(keep.tile([P, R], F32, name="picked%d" % i) for i in range(1, TILES))
-        shift = reuse.tile([P, 1], F32, name="shift", offset=24576)
-        neg_max = [shift] * TILES
-        sums = per_tile("sums", [P, 1], F32)
-        total = [z[2][:, S : S + 1], z[3][:, S : S + 1], sums[2][:], sums[3][:]]
-        inv = per_tile("inv", [P, 1], F32)
-        e = [reuse.tile([P, S], F32, name="e0", offset=10240)]
-        e.extend(keep.tile([P, S], F32, name="e%d" % i) for i in range(1, TILES))
-        prob = per_tile("prob", [P, S], F32)
+        free = (None,) * TILES
+        h_raw = placed("h_raw", [P, PACK, P], F32, (None, 0, 4032, 8096))
+        h_bf = placed("h_bf", [P, P, PACK], BF16, (7104, None, None, 12288), align_bytes=64)
+        h_codes = placed("h_codes", [P, P], U32, free, align_bytes=64)
+        h_bytes = placed("h_bytes", [P, P], U8, free, align_bytes=64)
+        counts_early = placed("counts", [P, R], F32, (2048, 6144))
+        counts_rest = reuse.tile([P, TILES - 2, R], F32, name="counts_rest", offset=25536)
+        counts = [counts_early[0][:], counts_early[1][:]] + [counts_rest[:, i, :] for i in range(TILES - 2)]
+        drop = placed("drop", [P, R], F32, (16320, 13248, 9184, 8192))
+        z = placed("z", [P, S], F32, (None, 17312, 14240, 10176))
+        lowered = placed("lowered", [P, R], F32, (None, 19392, 21440, 23488))
+        e = placed("e", [P, S], F32, (19392, 21440, 23488, None))
+        neg_max = placed("neg_max", [P, 1], F32, (8128, 9216, 8224, None))
+        total = placed("total", [P, 1], F32, free)
+        inv = placed("inv", [P, 1], F32, (9248, 8256, None, None))
+        prob = placed("prob", [P, S], F32, free)
 
         def load_h(u):
             nc.sync.dma_start(
                 out=h_raw[u][:], in_=hT[:, u * P : (u + 1) * P].rearrange("(p j) w -> p j w", j=PACK)
             )
 
-        def cast(u):
-            nc.scalar.activation(
+        def cast_views(u):
+            return dict(
                 out=h_bf[u][:].rearrange("p (c w) j -> p c j w", w=4),
                 in_=h_raw[u][:].rearrange("p j (c w) -> p c j w", w=4),
-                func=ACT.Copy,
             )
 
         def quantize_h(u):
@@ -90,7 +79,9 @@ def tile_picked_yrepp_pen_p_kernel(tc, x_words, x_scales, hT, cnt, offs, hist, o
             )
 
         def penalty(i):
-            nc.scalar.activation(out=drop[i][:], in_=counts[i], func=ACT.Copy, scale=-0.3, bias=-0.2)
+            nc.vector.tensor_scalar(
+                out=drop[i][:], in0=counts[i], scalar1=-0.3, scalar2=-0.2, op0=ALU.mult, op1=ALU.add
+            )
 
         def product(i, lo, hi):
             acc = psum.tile([P, hi - lo], F32, name="acc%d_%d" % (i, lo))
@@ -105,34 +96,34 @@ def tile_picked_yrepp_pen_p_kernel(tc, x_words, x_scales, hT, cnt, offs, hist, o
             )
             return acc
 
-        def empty(i, lo, hi, acc):
-            nc.scalar.activation(out=z[i][:, lo:hi], in_=acc[:], func=ACT.Copy)
+        def first_logits(lo, hi):
+            nc.scalar.activation(out=z[0][:, lo:hi], in_=product(0, lo, hi)[:], func=ACT.Copy)
 
-        def logits(i, lo, hi):
-            empty(i, lo, hi, product(i, lo, hi))
+        def logits(i):
+            nc.vector.tensor_copy(out=z[i][:], in_=product(i, 0, S)[:])
 
         def gather(i):
-            nc.vector.tensor_copy(out=picked[i][:], in_=z[i][:, 0:S].indirect(hist_sb[:]))
+            nc.vector.tensor_tensor(out=lowered[i][:], in0=z[i][:].indirect(hist_sb[:]), in1=drop[i][:], op=ALU.add)
 
         def scatter(i):
-            nc.vector.tensor_tensor(out=z[i][:].indirect(hist_sb[:]), in0=picked[i][:], in1=drop[i][:], op=ALU.add)
+            nc.scalar.activation(out=z[i][:].indirect(hist_sb[:]), in_=lowered[i][:], func=ACT.Copy)
 
         def row_max(i):
-            nc.vector.tensor_reduce(out=neg_max[i][:], in_=z[i][:, 0:S], axis=AXIS.X, op=ALU.max, negate=True)
-            nc.scalar.activation(out=e[i][:], in_=z[i][:, 0:S], func=ACT.Exp, bias=neg_max[i][:], accum_out=total[i])
+            nc.vector.tensor_reduce(out=neg_max[i][:], in_=z[i][:], axis=AXIS.X, op=ALU.max, negate=True)
 
-        def finish(i):
-            nc.vector.reciprocal(out=inv[i][:], in_=total[i])
-            if i < TILES - 1:
-                nc.scalar.activation(out=prob[i][:], in_=e[i][:], func=ACT.Copy, scale=inv[i][:])
-                nc.sync.dma_start(out=out[i * P : (i + 1) * P, :], in_=prob[i][:])
-            else:
-                rows = slice(i * P, (i + 1) * P)
-                nc.scalar.activation(out=prob[i][:, :HALF], in_=e[i][:, :HALF], func=ACT.Copy, scale=inv[i][:])
-                nc.vector.tensor_scalar(
-                    out=prob[i][:, HALF:], in0=e[i][:, HALF:], scalar1=inv[i][:], scalar2=None, op0=ALU.mult
-                )
-                nc.sync.dma_start(out=out[rows, :], in_=prob[i][:])
+        def exponential(i):
+            nc.scalar.activation(out=e[i][:], in_=z[i][:], func=ACT.Exp, bias=neg_max[i][:], accum_out=total[i][:])
+
+        def inverse(i):
+            nc.vector.reciprocal(out=inv[i][:], in_=total[i][:])
+
+        def normalise(i, lo):
+            nc.vector.tensor_scalar(
+                out=prob[i][:, lo:], in0=e[i][:, lo:], scalar1=inv[i][:], scalar2=None, op0=ALU.mult
+            )
+            if lo:
+                nc.scalar.activation(out=prob[i][:, :lo], in_=e[i][:, :lo], func=ACT.Copy, scale=inv[i][:])
+            nc.sync.dma_start(out=out[i * P : (i + 1) * P, :], in_=prob[i][:])
 
         nc.scalar.dma_start(out=scale_table[16:32, :].bitcast(I32), in_=x_scales[0].bitcast(I32))
         nc.sync.dma_start(offs_sb[:], offs)
@@ -150,49 +141,56 @@ def tile_picked_yrepp_pen_p_kernel(tc, x_words, x_scales, hT, cnt, offs, hist, o
                 in_=picked_bytes[16 + 4 * q : 20 + 4 * q, :].bitcast(I32),
             )
         load_h(1)
-
-        cast(0)
-        quantize_h(0)
+        nc.sync.dma_start(out=counts[0], in_=cnt[0:P, :])
         load_h(2)
-        nc.sync.dma_start(out=counts_first[:], in_=cnt[0:P, :])
+
+        nc.scalar.activation(func=ACT.Copy, **cast_views(0))
+        quantize_h(0)
+        nc.sync.dma_start(out=counts[1], in_=cnt[P : 2 * P, :])
+        load_h(3)
+        nc.sync.dma_start(out=counts_rest[:], in_=cnt[2 * P :, :].rearrange("(i p) r -> p i r", p=P))
         for lo in (0, HALF):
             nc.vector.tensor_copy(
                 out=x_codes[:, lo : lo + HALF], in_=word_table[:].indirect(offs_sb[:, lo // 16 : (lo + HALF) // 16])
             )
             if lo == 0:
-                logits(0, 0, HALF)
-        nc.vector.tensor_copy(
-            out=h_bf[1][:].rearrange("p (c w) j -> p c j w", w=4), in_=h_raw[1][:].rearrange("p j (c w) -> p c j w", w=4)
-        )
-        logits(0, HALF, HALF + P)
-        logits(0, HALF + P, S)
-        load_h(3)
-        nc.sync.dma_start(out=counts_second[:], in_=cnt[P : 2 * P, :])
+                first_logits(0, HALF)
+        first_logits(HALF, HALF + P)
+        first_logits(HALF + P, S)
+        nc.vector.tensor_copy(**cast_views(1))
+        penalty(0)
         quantize_h(1)
-        nc.vector.tensor_scalar(
-            out=drop[0][:, :SPLIT], in0=counts[0][:, :SPLIT], scalar1=-0.3, scalar2=-0.2, op0=ALU.mult, op1=ALU.add
-        )
-        cast(2)
-        nc.scalar.activation(out=drop[0][:, SPLIT:], in_=counts[0][:, SPLIT:], func=ACT.Copy, scale=-0.3, bias=-0.2)
-        nc.sync.dma_start(out=counts_rest[:], in_=cnt[2 * P :, :].rearrange("(i p) r -> p i r", p=P))
+        nc.scalar.activation(func=ACT.Copy, **cast_views(2))
         gather(0)
-        quantize_h(2)
-        logits(1, 0, S)
-        cast(3)
+        scatter(0)
+        logits(1)
         penalty(1)
-        for i in range(TILES):
-            scatter(i)
-            if i > 0:
-                finish(i - 1)
-            if i + 1 < TILES:
-                gather(i + 1)
-            if i == 0:
-                quantize_h(3)
-                acc = [product(2, 0, S), product(3, 0, S)]
-                empty(2, 0, S, acc[0])
-            row_max(i)
-            if i == 0:
-                empty(3, 0, S, acc[1])
-            if i + 2 < TILES:
-                penalty(i + 2)
-        finish(TILES - 1)
+        quantize_h(2)
+        gather(1)
+        scatter(1)
+        nc.vector.tensor_copy(**cast_views(3))
+        logits(2)
+        row_max(0)
+        exponential(0)
+        penalty(2)
+        quantize_h(3)
+        gather(2)
+        scatter(2)
+        row_max(1)
+        exponential(1)
+        logits(3)
+        inverse(0)
+        penalty(3)
+        gather(3)
+        scatter(3)
+        normalise(0, 0)
+        row_max(2)
+        exponential(2)
+        inverse(1)
+        normalise(1, 0)
+        row_max(3)
+        exponential(3)
+        inverse(2)
+        normalise(2, 0)
+        inverse(3)
+        normalise(3, HALF)

@@ -46,25 +46,29 @@ def tile_picked_yrepp_pen_p_kernel(tc, x_words, x_scales, hT, cnt, offs, hist, o
         x_bytes = keep.tile([P, S], U8, name="x_bytes", align_bytes=64)
 
         free = (None,) * TILES
-        h_raw = placed("h_raw", [P, PACK, P], F32, (None, 0, 4032, 8096))
-        h_bf = placed("h_bf", [P, P, PACK], BF16, (7104, None, None, 12288), align_bytes=64)
+        h_raw = placed("h_raw", [P, PACK, P], F32, (None, 0, 6144, 9120))
+        h_bf = placed("h_bf", [P, P, PACK], BF16, (8128, None, 11264, 11264), align_bytes=64)
         h_codes = placed("h_codes", [P, P], U32, free, align_bytes=64)
         h_bytes = placed("h_bytes", [P, P], U8, free, align_bytes=64)
-        counts_early = placed("counts", [P, R], F32, (2048, 6144))
-        counts_rest = reuse.tile([P, TILES - 2, R], F32, name="counts_rest", offset=25536)
-        counts = [counts_early[0][:], counts_early[1][:]] + [counts_rest[:, i, :] for i in range(TILES - 2)]
-        drop = placed("drop", [P, R], F32, (16320, 13248, 9184, 8192))
-        z = placed("z", [P, S], F32, (None, 17312, 14240, 10176))
-        lowered = placed("lowered", [P, R], F32, (None, 19392, 21440, 23488))
-        e = placed("e", [P, S], F32, (19392, 21440, 23488, None))
-        neg_max = placed("neg_max", [P, 1], F32, (8128, 9216, 8224, None))
+        counts = placed("counts", [P, 2, R], F32, (4032, 25536))
+        drop = placed("drop", [P, 2, R], F32, (12288, 9184))
+        z = placed("z", [P, S], F32, (14336, None, None, 14336))
+        lowered = placed("lowered", [P, R], F32, free)
+        e = placed("e", [P, S], F32, free)
+        shifts = placed("shift", [P, 1], F32, (12288, None))
+        neg_max = [shifts[i // (TILES - 1)] for i in range(TILES)]
         total = placed("total", [P, 1], F32, free)
-        inv = placed("inv", [P, 1], F32, (9248, 8256, None, None))
+        inv = placed("inv", [P, 1], F32, free)
         prob = placed("prob", [P, S], F32, free)
 
         def load_h(u):
             nc.sync.dma_start(
                 out=h_raw[u][:], in_=hT[:, u * P : (u + 1) * P].rearrange("(p j) w -> p j w", j=PACK)
+            )
+
+        def load_counts(j):
+            nc.sync.dma_start(
+                out=counts[j][:], in_=cnt[2 * j * P : 2 * (j + 1) * P, :].rearrange("(i p) r -> p i r", p=P)
             )
 
         def cast_views(u):
@@ -78,9 +82,9 @@ def tile_picked_yrepp_pen_p_kernel(tc, x_words, x_scales, hT, cnt, offs, hist, o
                 out=h_codes[u][:].bitcast(FP8X4), scales=h_bytes[u][:], in_=h_bf[u][:].rearrange("p w j -> p (w j)")
             )
 
-        def penalty(i):
+        def penalty(j):
             nc.vector.tensor_scalar(
-                out=drop[i][:], in0=counts[i], scalar1=-0.3, scalar2=-0.2, op0=ALU.mult, op1=ALU.add
+                out=drop[j][:], in0=counts[j][:], scalar1=-0.3, scalar2=-0.2, op0=ALU.mult, op1=ALU.add
             )
 
         def product(i, lo, hi):
@@ -103,7 +107,7 @@ def tile_picked_yrepp_pen_p_kernel(tc, x_words, x_scales, hT, cnt, offs, hist, o
             nc.vector.tensor_copy(out=z[i][:], in_=product(i, 0, S)[:])
 
         def gather(i):
-            nc.vector.tensor_tensor(out=lowered[i][:], in0=z[i][:].indirect(hist_sb[:]), in1=drop[i][:], op=ALU.add)
+            nc.vector.tensor_tensor(out=lowered[i][:], in0=z[i][:].indirect(hist_sb[:]), in1=drop[i // 2][:, i % 2, :], op=ALU.add)
 
         def scatter(i):
             nc.scalar.activation(out=z[i][:].indirect(hist_sb[:]), in_=lowered[i][:], func=ACT.Copy)
@@ -127,9 +131,9 @@ def tile_picked_yrepp_pen_p_kernel(tc, x_words, x_scales, hT, cnt, offs, hist, o
 
         nc.scalar.dma_start(out=scale_table[16:32, :].bitcast(I32), in_=x_scales[0].bitcast(I32))
         nc.sync.dma_start(offs_sb[:], offs)
+        nc.sync.dma_start(hist_sb[:], hist)
         load_h(0)
         nc.sync.dma_start(out=word_table[:].bitcast(I32), in_=x_words[0].rearrange("p n t -> p (n t)").bitcast(I32))
-        nc.sync.dma_start(hist_sb[:], hist)
         for lo, hi in ((0, 16), (32, 64), (64, P)):
             nc.vector.memset(scale_table[lo:hi, :].bitcast(I32), 0)
         nc.vector.memset(x_bytes[:].bitcast(I32), 0)
@@ -141,14 +145,13 @@ def tile_picked_yrepp_pen_p_kernel(tc, x_words, x_scales, hT, cnt, offs, hist, o
                 in_=picked_bytes[16 + 4 * q : 20 + 4 * q, :].bitcast(I32),
             )
         load_h(1)
-        nc.sync.dma_start(out=counts[0], in_=cnt[0:P, :])
-        load_h(2)
+        load_counts(0)
 
         nc.scalar.activation(func=ACT.Copy, **cast_views(0))
         quantize_h(0)
-        nc.sync.dma_start(out=counts[1], in_=cnt[P : 2 * P, :])
+        load_h(2)
         load_h(3)
-        nc.sync.dma_start(out=counts_rest[:], in_=cnt[2 * P :, :].rearrange("(i p) r -> p i r", p=P))
+        load_counts(1)
         for lo in (0, HALF):
             nc.vector.tensor_copy(
                 out=x_codes[:, lo : lo + HALF], in_=word_table[:].indirect(offs_sb[:, lo // 16 : (lo + HALF) // 16])
@@ -164,15 +167,14 @@ def tile_picked_yrepp_pen_p_kernel(tc, x_words, x_scales, hT, cnt, offs, hist, o
         gather(0)
         scatter(0)
         logits(1)
-        penalty(1)
         quantize_h(2)
         gather(1)
         scatter(1)
-        nc.vector.tensor_copy(**cast_views(3))
         logits(2)
+        nc.vector.tensor_copy(**cast_views(3))
         row_max(0)
         exponential(0)
-        penalty(2)
+        penalty(1)
         quantize_h(3)
         gather(2)
         scatter(2)
@@ -180,7 +182,6 @@ def tile_picked_yrepp_pen_p_kernel(tc, x_words, x_scales, hT, cnt, offs, hist, o
         exponential(1)
         logits(3)
         inverse(0)
-        penalty(3)
         gather(3)
         scatter(3)
         normalise(0, 0)

@@ -46,29 +46,25 @@ def tile_picked_yrepp_pen_p_kernel(tc, x_words, x_scales, hT, cnt, offs, hist, o
         x_bytes = keep.tile([P, S], U8, name="x_bytes", align_bytes=64)
 
         free = (None,) * TILES
-        h_raw = placed("h_raw", [P, PACK, P], F32, (None, 0, 6144, 9120))
-        h_bf = placed("h_bf", [P, P, PACK], BF16, (8128, None, 11264, 11264), align_bytes=64)
-        h_codes = placed("h_codes", [P, P], U32, free, align_bytes=64)
+        h_raw = placed("h_raw", [P, PACK, P], F32, (None, None, 0, 4032))
+        h_bf = placed("h_bf", [P, P, PACK], BF16, (8128, None, None, None), align_bytes=64)
+        h_codes = placed("h_codes", [P, P], U32, (None, None, 12288, None), align_bytes=64)
         h_bytes = placed("h_bytes", [P, P], U8, free, align_bytes=64)
-        counts = placed("counts", [P, 2, R], F32, (4032, 25536))
-        drop = placed("drop", [P, 2, R], F32, (12288, 9184))
-        z = placed("z", [P, S], F32, (14336, None, None, 14336))
-        lowered = placed("lowered", [P, R], F32, free)
+        counts_first = keep.tile([P, R], F32, name="counts_first")
+        counts_rest = reuse.tile([P, TILES - 1, R], F32, name="counts_rest", offset=9120)
+        counts = [counts_first[:]] + [counts_rest[:, i, :] for i in range(TILES - 1)]
+        drop = placed("drop", [P, R], F32, (None, 13312, 14336, None))
+        z = placed("z", [P, S], F32, free)
+        lowered = placed("lowered", [P, R], F32, (None, 12288, None, None))
         e = placed("e", [P, S], F32, free)
-        shifts = placed("shift", [P, 1], F32, (12288, None))
-        neg_max = [shifts[i // (TILES - 1)] for i in range(TILES)]
-        total = placed("total", [P, 1], F32, free)
-        inv = placed("inv", [P, 1], F32, free)
+        neg_max = [t[:] for t in placed("shift", [P, 1], F32, (13312, 14336, 17408, 13312))]
+        total = placed("total", [P, 1], F32, (17408, None, None, None))
+        inv = placed("inv", [P, 1], F32, (14400, None, None, None))
         prob = placed("prob", [P, S], F32, free)
 
         def load_h(u):
             nc.sync.dma_start(
                 out=h_raw[u][:], in_=hT[:, u * P : (u + 1) * P].rearrange("(p j) w -> p j w", j=PACK)
-            )
-
-        def load_counts(j):
-            nc.sync.dma_start(
-                out=counts[j][:], in_=cnt[2 * j * P : 2 * (j + 1) * P, :].rearrange("(i p) r -> p i r", p=P)
             )
 
         def cast_views(u):
@@ -82,9 +78,9 @@ def tile_picked_yrepp_pen_p_kernel(tc, x_words, x_scales, hT, cnt, offs, hist, o
                 out=h_codes[u][:].bitcast(FP8X4), scales=h_bytes[u][:], in_=h_bf[u][:].rearrange("p w j -> p (w j)")
             )
 
-        def penalty(j):
+        def penalty(i):
             nc.vector.tensor_scalar(
-                out=drop[j][:], in0=counts[j][:], scalar1=-0.3, scalar2=-0.2, op0=ALU.mult, op1=ALU.add
+                out=drop[i][:], in0=counts[i], scalar1=-0.3, scalar2=-0.2, op0=ALU.mult, op1=ALU.add
             )
 
         def product(i, lo, hi):
@@ -107,26 +103,33 @@ def tile_picked_yrepp_pen_p_kernel(tc, x_words, x_scales, hT, cnt, offs, hist, o
             nc.vector.tensor_copy(out=z[i][:], in_=product(i, 0, S)[:])
 
         def gather(i):
-            nc.vector.tensor_tensor(out=lowered[i][:], in0=z[i][:].indirect(hist_sb[:]), in1=drop[i // 2][:, i % 2, :], op=ALU.add)
+            nc.vector.tensor_tensor(out=lowered[i][:], in0=z[i][:].indirect(hist_sb[:]), in1=drop[i][:], op=ALU.add)
 
         def scatter(i):
             nc.scalar.activation(out=z[i][:].indirect(hist_sb[:]), in_=lowered[i][:], func=ACT.Copy)
 
+        def plain_gather(i):
+            nc.vector.tensor_copy(out=lowered[i][:], in_=z[i][:].indirect(hist_sb[:]))
+
+        def fused_scatter(i):
+            nc.vector.tensor_tensor(out=z[i][:].indirect(hist_sb[:]), in0=lowered[i][:], in1=drop[i][:], op=ALU.add)
+
         def row_max(i):
-            nc.vector.tensor_reduce(out=neg_max[i][:], in_=z[i][:], axis=AXIS.X, op=ALU.max, negate=True)
+            nc.vector.tensor_reduce(out=neg_max[i], in_=z[i][:], axis=AXIS.X, op=ALU.max, negate=True)
 
         def exponential(i):
-            nc.scalar.activation(out=e[i][:], in_=z[i][:], func=ACT.Exp, bias=neg_max[i][:], accum_out=total[i][:])
+            nc.scalar.activation(out=e[i][:], in_=z[i][:], func=ACT.Exp, bias=neg_max[i], accum_out=total[i][:])
 
         def inverse(i):
             nc.vector.reciprocal(out=inv[i][:], in_=total[i][:])
 
-        def normalise(i, lo):
-            nc.vector.tensor_scalar(
-                out=prob[i][:, lo:], in0=e[i][:, lo:], scalar1=inv[i][:], scalar2=None, op0=ALU.mult
-            )
-            if lo:
-                nc.scalar.activation(out=prob[i][:, :lo], in_=e[i][:, :lo], func=ACT.Copy, scale=inv[i][:])
+        def normalise(i, cut):
+            if cut < S:
+                nc.vector.tensor_scalar(
+                    out=prob[i][:, cut:], in0=e[i][:, cut:], scalar1=inv[i][:], scalar2=None, op0=ALU.mult
+                )
+            if cut > 0:
+                nc.scalar.activation(out=prob[i][:, :cut], in_=e[i][:, :cut], func=ACT.Copy, scale=inv[i][:])
             nc.sync.dma_start(out=out[i * P : (i + 1) * P, :], in_=prob[i][:])
 
         nc.scalar.dma_start(out=scale_table[16:32, :].bitcast(I32), in_=x_scales[0].bitcast(I32))
@@ -134,6 +137,8 @@ def tile_picked_yrepp_pen_p_kernel(tc, x_words, x_scales, hT, cnt, offs, hist, o
         nc.sync.dma_start(hist_sb[:], hist)
         load_h(0)
         nc.sync.dma_start(out=word_table[:].bitcast(I32), in_=x_words[0].rearrange("p n t -> p (n t)").bitcast(I32))
+        load_h(1)
+        nc.sync.dma_start(out=counts[0], in_=cnt[0:P, :])
         for lo, hi in ((0, 16), (32, 64), (64, P)):
             nc.vector.memset(scale_table[lo:hi, :].bitcast(I32), 0)
         nc.vector.memset(x_bytes[:].bitcast(I32), 0)
@@ -144,54 +149,54 @@ def tile_picked_yrepp_pen_p_kernel(tc, x_words, x_scales, hT, cnt, offs, hist, o
                 out=x_bytes[32 * q : 32 * q + 4, :].bitcast(I32),
                 in_=picked_bytes[16 + 4 * q : 20 + 4 * q, :].bitcast(I32),
             )
-        load_h(1)
-        load_counts(0)
+        load_h(2)
+        load_h(3)
 
         nc.scalar.activation(func=ACT.Copy, **cast_views(0))
         quantize_h(0)
-        load_h(2)
-        load_h(3)
-        load_counts(1)
+        nc.sync.dma_start(out=counts_rest[:], in_=cnt[P:, :].rearrange("(i p) r -> p i r", p=P))
+        nc.scalar.activation(func=ACT.Copy, **cast_views(1))
         for lo in (0, HALF):
             nc.vector.tensor_copy(
                 out=x_codes[:, lo : lo + HALF], in_=word_table[:].indirect(offs_sb[:, lo // 16 : (lo + HALF) // 16])
             )
-            if lo == 0:
-                first_logits(0, HALF)
-        first_logits(HALF, HALF + P)
+        first_logits(0, HALF)
+        third_quarter = product(0, HALF, HALF + P)
         first_logits(HALF + P, S)
-        nc.vector.tensor_copy(**cast_views(1))
-        penalty(0)
         quantize_h(1)
-        nc.scalar.activation(func=ACT.Copy, **cast_views(2))
+        penalty(0)
+        nc.vector.tensor_copy(out=z[0][:, HALF : HALF + P], in_=third_quarter[:])
+        nc.scalar.activation(out=z[1][:], in_=product(1, 0, S)[:], func=ACT.Copy)
         gather(0)
         scatter(0)
-        logits(1)
+        nc.vector.tensor_copy(**cast_views(2))
+        nc.vector.tensor_copy(**cast_views(3))
         quantize_h(2)
+        nc.scalar.activation(out=z[2][:], in_=product(2, 0, S)[:], func=ACT.Copy)
+        quantize_h(3)
+        penalty(1)
+        penalty(2)
+        penalty(3)
         gather(1)
         scatter(1)
-        logits(2)
-        nc.vector.tensor_copy(**cast_views(3))
+        logits(3)
         row_max(0)
         exponential(0)
-        penalty(1)
-        quantize_h(3)
+        plain_gather(3)
         gather(2)
         scatter(2)
+        fused_scatter(3)
         row_max(1)
         exponential(1)
-        logits(3)
         inverse(0)
-        gather(3)
-        scatter(3)
-        normalise(0, 0)
-        row_max(2)
-        exponential(2)
-        inverse(1)
-        normalise(1, 0)
         row_max(3)
         exponential(3)
-        inverse(2)
-        normalise(2, 0)
+        normalise(0, 0)
+        inverse(1)
+        row_max(2)
+        exponential(2)
+        normalise(1, 0)
         inverse(3)
-        normalise(3, HALF)
+        normalise(3, 0)
+        inverse(2)
+        normalise(2, HALF)

@@ -191,10 +191,13 @@ def tile_picked_yrepp_pen_p_kernel(tc, x_words, x_scales, hT, cnt, offs, hist, o
         inverse(0)
         row_max(3)
         exponential(3)
-        normalise(0, 0)
-        inverse(1)
+        nc.gpsimd.tensor_scalar(
+            out=prob[0][:], in0=e[0][:], scalar1=inv[0][:], scalar2=0.0, op0=ALU.mult, op1=ALU.add
+        )
+        nc.sync.dma_start(out=out[0:P, :], in_=prob[0][:])
         row_max(2)
         exponential(2)
+        inverse(1)
         normalise(1, 0)
         inverse(3)
         normalise(3, 0)

@@ -53,9 +53,9 @@ def tile_picked_yrepp_pen_p_kernel(tc, x_words, x_scales, hT, cnt, offs, hist, o
         counts_first = keep.tile([P, R], F32, name="counts_first")
         counts_rest = reuse.tile([P, TILES - 1, R], F32, name="counts_rest", offset=9120)
         counts = [counts_first[:]] + [counts_rest[:, i, :] for i in range(TILES - 1)]
-        drop = placed("drop", [P, R], F32, (None, 13312, 14336, None))
+        drop = placed("drop", [P, R], F32, (12288, 13312, 14336, None))
         z = placed("z", [P, S], F32, free)
-        lowered = placed("lowered", [P, R], F32, (None, 12288, None, None))
+        lowered = placed("lowered", [P, R], F32, (None, None, None, None))
         e = placed("e", [P, S], F32, free)
         neg_max = [t[:] for t in placed("shift", [P, 1], F32, (13312, 14336, 17408, 13312))]
         total = placed("total", [P, 1], F32, (17408, None, None, None))

@@ -43,21 +43,25 @@ def tile_picked_yrepp_pen_p_kernel(tc, x_words, x_scales, hT, cnt, offs, hist, o
         scale_table = reuse.tile([P, T], U8, name="scale_table", offset=2016)
         picked_bytes = reuse.tile([P, S], U8, name="picked_bytes", offset=25536)
         x_codes = keep.tile([P, S], U32, name="x_codes", align_bytes=64)
-        x_bytes = keep.tile([P, S], U8, name="x_bytes", align_bytes=64)
+        x_bytes = reuse.tile([P, S], U8, name="x_bytes", offset=22528, align_bytes=64)
 
         free = (None,) * TILES
         h_raw = placed("h_raw", [P, PACK, P], F32, (None, None, 0, 4032))
-        h_bf = placed("h_bf", [P, P, PACK], BF16, (8128, None, None, None), align_bytes=64)
-        h_codes = placed("h_codes", [P, P], U32, (None, None, 12288, None), align_bytes=64)
+        h_bf = placed("h_bf", [P, P, PACK], BF16, (8128, None, 20480, None), align_bytes=64)
+        h_codes = placed("h_codes", [P, P], U32, (None, None, 12288, 20480), align_bytes=64)
         h_bytes = placed("h_bytes", [P, P], U8, free, align_bytes=64)
         counts_first = keep.tile([P, R], F32, name="counts_first")
-        counts_rest = reuse.tile([P, TILES - 1, R], F32, name="counts_rest", offset=9120)
-        counts = [counts_first[:]] + [counts_rest[:, i, :] for i in range(TILES - 1)]
-        drop = placed("drop", [P, R], F32, (12288, 13312, 14336, None))
+        counts_second = reuse.tile([P, R], F32, name="counts_second", offset=9120)
+        counts_last = reuse.tile([P, 2, R], F32, name="counts_last", offset=6112)
+        counts = [counts_first[:], counts_second[:]]
+        drop_first = placed("drop", [P, R], F32, (12288, 13312))
+        drop_last = reuse.tile([P, 2, R], F32, name="drop_last", offset=14304)
+        drop = [drop_first[0][:], drop_first[1][:], drop_last[:, 0, :], drop_last[:, 1, :]]
         z = placed("z", [P, S], F32, free)
         lowered = placed("lowered", [P, R], F32, (None, None, None, None))
         e = placed("e", [P, S], F32, free)
-        neg_max = [t[:] for t in placed("shift", [P, 1], F32, (13312, 14336, 17408, 13312))]
+        first_shift = reuse.tile([P, 16], F32, name="first_shift", offset=22528)
+        neg_max = [first_shift[:, 0:1]] + [t[:] for t in placed("shift", [P, 1], F32, (22560, 17408, 22528))]
         total = placed("total", [P, 1], F32, (17408, None, None, None))
         inv = placed("inv", [P, 1], F32, (14400, None, None, None))
         prob = placed("prob", [P, S], F32, free)
@@ -78,15 +82,12 @@ def tile_picked_yrepp_pen_p_kernel(tc, x_words, x_scales, hT, cnt, offs, hist, o
                 out=h_codes[u][:].bitcast(FP8X4), scales=h_bytes[u][:], in_=h_bf[u][:].rearrange("p w j -> p (w j)")
             )
 
-        def penalty(i):
-            nc.vector.tensor_scalar(
-                out=drop[i][:], in0=counts[i], scalar1=-0.3, scalar2=-0.2, op0=ALU.mult, op1=ALU.add
-            )
+        def penalty(dst, src):
+            nc.vector.tensor_scalar(out=dst, in0=src, scalar1=-0.3, scalar2=-0.2, op0=ALU.mult, op1=ALU.add)
 
-        def product(i, lo, hi):
-            acc = psum.tile([P, hi - lo], F32, name="acc%d_%d" % (i, lo))
+        def multiply(acc, i, lo, hi):
             nc.tensor.matmul_mx(
-                out=acc[:],
+                out=acc,
                 lhsT=h_codes[i][:].bitcast(FP8X4),
                 lhsT_scale=h_bytes[i][:],
                 rhs=x_codes[:, lo:hi].bitcast(FP8X4),
@@ -94,16 +95,21 @@ def tile_picked_yrepp_pen_p_kernel(tc, x_words, x_scales, hT, cnt, offs, hist, o
                 start=True,
                 stop=True,
             )
+
+        def product(i, lo, hi):
+            acc = psum.tile([P, hi - lo], F32, name="acc%d_%d" % (i, lo))
+            multiply(acc[:], i, lo, hi)
             return acc
 
         def first_logits(lo, hi):
             nc.scalar.activation(out=z[0][:, lo:hi], in_=product(0, lo, hi)[:], func=ACT.Copy)
 
         def logits(i):
-            nc.vector.tensor_copy(out=z[i][:], in_=product(i, 0, S)[:])
+            for lo in (0, HALF):
+                nc.vector.tensor_copy(out=z[i][:, lo : lo + HALF], in_=product(i, lo, lo + HALF)[:])
 
         def gather(i):
-            nc.vector.tensor_tensor(out=lowered[i][:], in0=z[i][:].indirect(hist_sb[:]), in1=drop[i][:], op=ALU.add)
+            nc.vector.tensor_tensor(out=lowered[i][:], in0=z[i][:].indirect(hist_sb[:]), in1=drop[i], op=ALU.add)
 
         def scatter(i):
             nc.scalar.activation(out=z[i][:].indirect(hist_sb[:]), in_=lowered[i][:], func=ACT.Copy)
@@ -112,7 +118,7 @@ def tile_picked_yrepp_pen_p_kernel(tc, x_words, x_scales, hT, cnt, offs, hist, o
             nc.vector.tensor_copy(out=lowered[i][:], in_=z[i][:].indirect(hist_sb[:]))
 
         def fused_scatter(i):
-            nc.vector.tensor_tensor(out=z[i][:].indirect(hist_sb[:]), in0=lowered[i][:], in1=drop[i][:], op=ALU.add)
+            nc.vector.tensor_tensor(out=z[i][:].indirect(hist_sb[:]), in0=lowered[i][:], in1=drop[i], op=ALU.add)
 
         def row_max(i):
             nc.vector.tensor_reduce(out=neg_max[i], in_=z[i][:], axis=AXIS.X, op=ALU.max, negate=True)
@@ -154,7 +160,8 @@ def tile_picked_yrepp_pen_p_kernel(tc, x_words, x_scales, hT, cnt, offs, hist, o
 
         nc.scalar.activation(func=ACT.Copy, **cast_views(0))
         quantize_h(0)
-        nc.sync.dma_start(out=counts_rest[:], in_=cnt[P:, :].rearrange("(i p) r -> p i r", p=P))
+        nc.sync.dma_start(out=counts[1], in_=cnt[P : 2 * P, :])
+        nc.sync.dma_start(out=counts_last[:], in_=cnt[2 * P :, :].rearrange("(i p) r -> p i r", p=P))
         nc.scalar.activation(func=ACT.Copy, **cast_views(1))
         for lo in (0, HALF):
             nc.vector.tensor_copy(
@@ -164,7 +171,7 @@ def tile_picked_yrepp_pen_p_kernel(tc, x_words, x_scales, hT, cnt, offs, hist, o
         third_quarter = product(0, HALF, HALF + P)
         first_logits(HALF + P, S)
         quantize_h(1)
-        penalty(0)
+        penalty(drop[0], counts[0])
         nc.vector.tensor_copy(out=z[0][:, HALF : HALF + P], in_=third_quarter[:])
         nc.scalar.activation(out=z[1][:], in_=product(1, 0, S)[:], func=ACT.Copy)
         gather(0)
@@ -173,12 +180,13 @@ def tile_picked_yrepp_pen_p_kernel(tc, x_words, x_scales, hT, cnt, offs, hist, o
         nc.vector.tensor_copy(**cast_views(3))
         quantize_h(2)
         nc.scalar.activation(out=z[2][:], in_=product(2, 0, S)[:], func=ACT.Copy)
+        penalty(drop[1], counts[1])
         quantize_h(3)
-        penalty(1)
-        penalty(2)
-        penalty(3)
         gather(1)
         scatter(1)
+        nc.gpsimd.tensor_scalar(
+            out=drop_last[:], in0=counts_last[:], scalar1=-0.3, scalar2=-0.2, op0=ALU.mult, op1=ALU.add
+        )
         logits(3)
         row_max(0)
         exponential(0)

@@ -163,10 +163,8 @@ def tile_picked_yrepp_pen_p_kernel(tc, x_words, x_scales, hT, cnt, offs, hist, o
         nc.sync.dma_start(out=counts[1], in_=cnt[P : 2 * P, :])
         nc.sync.dma_start(out=counts_last[:], in_=cnt[2 * P :, :].rearrange("(i p) r -> p i r", p=P))
         nc.scalar.activation(func=ACT.Copy, **cast_views(1))
-        for lo in (0, HALF):
-            nc.vector.tensor_copy(
-                out=x_codes[:, lo : lo + HALF], in_=word_table[:].indirect(offs_sb[:, lo // 16 : (lo + HALF) // 16])
-            )
+        for lo, hi in ((0, HALF + P), (HALF + P, S)):
+            nc.vector.tensor_copy(out=x_codes[:, lo:hi], in_=word_table[:].indirect(offs_sb[:, lo // 16 : hi // 16]))
         first_logits(0, HALF)
         third_quarter = product(0, HALF, HALF + P)
         first_logits(HALF + P, S)

@@ -47,8 +47,8 @@ def tile_picked_yrepp_pen_p_kernel(tc, x_words, x_scales, hT, cnt, offs, hist, o
 
         free = (None,) * TILES
         h_raw = placed("h_raw", [P, PACK, P], F32, (None, None, 0, 4032))
-        h_bf = placed("h_bf", [P, P, PACK], BF16, (8128, None, 20480, None), align_bytes=64)
-        h_codes = placed("h_codes", [P, P], U32, (None, None, 12288, 20480), align_bytes=64)
+        h_bf = placed("h_bf", [P, P, PACK], BF16, (8128, None, None, None), align_bytes=64)
+        h_codes = placed("h_codes", [P, P], U32, (None, None, 12288, None), align_bytes=64)
         h_bytes = placed("h_bytes", [P, P], U8, free, align_bytes=64)
         counts_first = keep.tile([P, R], F32, name="counts_first")
         counts_second = reuse.tile([P, R], F32, name="counts_second", offset=9120)
@@ -63,7 +63,7 @@ def tile_picked_yrepp_pen_p_kernel(tc, x_words, x_scales, hT, cnt, offs, hist, o
         first_shift = reuse.tile([P, 16], F32, name="first_shift", offset=22528)
         neg_max = [first_shift[:, 0:1]] + [t[:] for t in placed("shift", [P, 1], F32, (22560, 17408, 22528))]
         total = placed("total", [P, 1], F32, (17408, None, None, None))
-        inv = placed("inv", [P, 1], F32, (14400, None, None, None))
+        inv = placed("inv", [P, 1], F32, free)
         prob = placed("prob", [P, S], F32, free)
 
         def load_h(u):
@@ -178,8 +178,8 @@ def tile_picked_yrepp_pen_p_kernel(tc, x_words, x_scales, hT, cnt, offs, hist, o
         nc.vector.tensor_copy(**cast_views(3))
         quantize_h(2)
         nc.scalar.activation(out=z[2][:], in_=product(2, 0, S)[:], func=ACT.Copy)
-        penalty(drop[1], counts[1])
         quantize_h(3)
+        penalty(drop[1], counts[1])
         gather(1)
         scatter(1)
         nc.gpsimd.tensor_scalar(
@@ -192,9 +192,9 @@ def tile_picked_yrepp_pen_p_kernel(tc, x_words, x_scales, hT, cnt, offs, hist, o
         gather(2)
         scatter(2)
         fused_scatter(3)
+        inverse(0)
         row_max(1)
         exponential(1)
-        inverse(0)
         row_max(3)
         exponential(3)
         nc.gpsimd.tensor_scalar(
@@ -208,4 +208,4 @@ def tile_picked_yrepp_pen_p_kernel(tc, x_words, x_scales, hT, cnt, offs, hist, o
         inverse(3)
         normalise(3, 0)
         inverse(2)
-        normalise(2, HALF)
+        normalise(2, P)

from contextlib import ExitStack

import concourse.mybir as mybir

K, T, S, V, R = 512, 2048, 512, 512, 256
FLOPS = 2 * K * V * S

F32 = mybir.dt.float32
BF16 = mybir.dt.bfloat16
I32 = mybir.dt.int32
U32 = mybir.dt.uint32
U16 = mybir.dt.uint16
U8 = mybir.dt.uint8
FP8X4 = mybir.dt.float8_e4m3fn_x4
ACT = mybir.ActivationFunctionType
ALU = mybir.AluOpType
AXIS = mybir.AxisListType

P = 128
PACK = 4
TILES = V // P
HALF = S // 2


def tile_picked_yrepp_pen_p_kernel(tc, x_words, x_scales, hT, cnt, offs, hist, out):
    nc = tc.nc
    with ExitStack() as ctx:
        keep = ctx.enter_context(tc.tile_pool(name="keep", bufs=1))
        psum = ctx.enter_context(tc.psum_pool(name="psum", bufs=1))
        reuse = ctx.enter_context(tc.tile_pool(name="reuse", bufs=1))

        def placed(name, shape, dtype, places, **kw):
            return [
                keep.tile(shape, dtype, name="%s%d" % (name, i), **kw)
                if at is None
                else reuse.tile(shape, dtype, name="%s%d" % (name, i), offset=at, **kw)
                for i, at in enumerate(places)
            ]

        offs_sb = keep.tile([P, S // 16], U16, name="offs_sb")
        hist_sb = keep.tile([P, R // 16], U16, name="hist_sb")
        word_table = keep.tile([P, T], U32, name="word_table")
        scale_table = reuse.tile([P, T], U8, name="scale_table", offset=2016)
        picked_bytes = reuse.tile([P, S], U8, name="picked_bytes", offset=25536)
        x_codes = keep.tile([P, S], U32, name="x_codes", align_bytes=64)
        x_bytes = reuse.tile([P, S], U8, name="x_bytes", offset=22528, align_bytes=64)

        free = (None,) * TILES
        h_raw = placed("h_raw", [P, PACK, P], F32, (None, None, 0, 4032))
        h_bf = placed("h_bf", [P, P, PACK], BF16, (8128, None, None, None), align_bytes=64)
        h_codes = placed("h_codes", [P, P], U32, (None, None, 12288, None), align_bytes=64)
        h_bytes = placed("h_bytes", [P, P], U8, free, align_bytes=64)
        counts_first = keep.tile([P, R], F32, name="counts_first")
        counts_second = reuse.tile([P, R], F32, name="counts_second", offset=9120)
        counts_last = reuse.tile([P, 2, R], F32, name="counts_last", offset=6112)
        counts = [counts_first[:], counts_second[:]]
        drop_first = placed("drop", [P, R], F32, (12288, 13312))
        drop_last = reuse.tile([P, 2, R], F32, name="drop_last", offset=14304)
        drop = [drop_first[0][:], drop_first[1][:], drop_last[:, 0, :], drop_last[:, 1, :]]
        z = placed("z", [P, S], F32, free)
        lowered = placed("lowered", [P, R], F32, (None, None, None, None))
        e = placed("e", [P, S], F32, free)
        first_shift = reuse.tile([P, 16], F32, name="first_shift", offset=22528)
        neg_max = [first_shift[:, 0:1]] + [t[:] for t in placed("shift", [P, 1], F32, (22560, 17408, 22528))]
        total = placed("total", [P, 1], F32, (17408, None, None, None))
        inv = placed("inv", [P, 1], F32, free)
        prob = placed("prob", [P, S], F32, free)

        def load_h(u):
            nc.sync.dma_start(
                out=h_raw[u][:], in_=hT[:, u * P : (u + 1) * P].rearrange("(p j) w -> p j w", j=PACK)
            )

        def cast_views(u):
            return dict(
                out=h_bf[u][:].rearrange("p (c w) j -> p c j w", w=4),
                in_=h_raw[u][:].rearrange("p j (c w) -> p c j w", w=4),
            )

        def quantize_h(u):
            nc.vector.quantize_mx(
                out=h_codes[u][:].bitcast(FP8X4), scales=h_bytes[u][:], in_=h_bf[u][:].rearrange("p w j -> p (w j)")
            )

        def penalty(dst, src):
            nc.vector.tensor_scalar(out=dst, in0=src, scalar1=-0.3, scalar2=-0.2, op0=ALU.mult, op1=ALU.add)

        def multiply(acc, i, lo, hi):
            nc.tensor.matmul_mx(
                out=acc,
                lhsT=h_codes[i][:].bitcast(FP8X4),
                lhsT_scale=h_bytes[i][:],
                rhs=x_codes[:, lo:hi].bitcast(FP8X4),
                rhs_scale=x_bytes[:, lo:hi],
                start=True,
                stop=True,
            )

        def product(i, lo, hi):
            acc = psum.tile([P, hi - lo], F32, name="acc%d_%d" % (i, lo))
            multiply(acc[:], i, lo, hi)
            return acc

        def first_logits(lo, hi):
            nc.scalar.activation(out=z[0][:, lo:hi], in_=product(0, lo, hi)[:], func=ACT.Copy)

        def logits(i):
            for lo in (0, HALF):
                nc.vector.tensor_copy(out=z[i][:, lo : lo + HALF], in_=product(i, lo, lo + HALF)[:])

        def gather(i):
            nc.vector.tensor_tensor(out=lowered[i][:], in0=z[i][:].indirect(hist_sb[:]), in1=drop[i], op=ALU.add)

        def scatter(i):
            nc.scalar.activation(out=z[i][:].indirect(hist_sb[:]), in_=lowered[i][:], func=ACT.Copy)

        def plain_gather(i):
            nc.vector.tensor_copy(out=lowered[i][:], in_=z[i][:].indirect(hist_sb[:]))

        def fused_scatter(i):
            nc.vector.tensor_tensor(out=z[i][:].indirect(hist_sb[:]), in0=lowered[i][:], in1=drop[i], op=ALU.add)

        def row_max(i):
            nc.vector.tensor_reduce(out=neg_max[i], in_=z[i][:], axis=AXIS.X, op=ALU.max, negate=True)

        def exponential(i):
            nc.scalar.activation(out=e[i][:], in_=z[i][:], func=ACT.Exp, bias=neg_max[i], accum_out=total[i][:])

        def inverse(i):
            nc.vector.reciprocal(out=inv[i][:], in_=total[i][:])

        def normalise(i, cut):
            if cut < S:
                nc.vector.tensor_scalar(
                    out=prob[i][:, cut:], in0=e[i][:, cut:], scalar1=inv[i][:], scalar2=None, op0=ALU.mult
                )
            if cut > 0:
                nc.scalar.activation(out=prob[i][:, :cut], in_=e[i][:, :cut], func=ACT.Copy, scale=inv[i][:])
            nc.sync.dma_start(out=out[i * P : (i + 1) * P, :], in_=prob[i][:])

        nc.scalar.dma_start(out=scale_table[16:32, :].bitcast(I32), in_=x_scales[0].bitcast(I32))
        nc.sync.dma_start(offs_sb[:], offs)
        nc.sync.dma_start(hist_sb[:], hist)
        load_h(0)
        nc.sync.dma_start(out=word_table[:].bitcast(I32), in_=x_words[0].rearrange("p n t -> p (n t)").bitcast(I32))
        load_h(1)
        nc.sync.dma_start(out=counts[0], in_=cnt[0:P, :])
        for lo, hi in ((0, 16), (32, 64), (64, P)):
            nc.vector.memset(scale_table[lo:hi, :].bitcast(I32), 0)
        nc.vector.memset(x_bytes[:].bitcast(I32), 0)

        nc.vector.tensor_copy(out=picked_bytes[:], in_=scale_table[:].indirect(offs_sb[:]))
        for q in range(4):
            nc.sync.dma_start(
                out=x_bytes[32 * q : 32 * q + 4, :].bitcast(I32),
                in_=picked_bytes[16 + 4 * q : 20 + 4 * q, :].bitcast(I32),
            )
        load_h(2)
        load_h(3)

        nc.scalar.activation(func=ACT.Copy, **cast_views(0))
        quantize_h(0)
        nc.sync.dma_start(out=counts[1], in_=cnt[P : 2 * P, :])
        nc.sync.dma_start(out=counts_last[:], in_=cnt[2 * P :, :].rearrange("(i p) r -> p i r", p=P))
        nc.scalar.activation(func=ACT.Copy, **cast_views(1))
        for lo, hi in ((0, HALF + P), (HALF + P, S)):
            nc.vector.tensor_copy(out=x_codes[:, lo:hi], in_=word_table[:].indirect(offs_sb[:, lo // 16 : hi // 16]))
        first_logits(0, HALF)
        third_quarter = product(0, HALF, HALF + P)
        first_logits(HALF + P, S)
        quantize_h(1)
        penalty(drop[0], counts[0])
        nc.vector.tensor_copy(out=z[0][:, HALF : HALF + P], in_=third_quarter[:])
        nc.scalar.activation(out=z[1][:], in_=product(1, 0, S)[:], func=ACT.Copy)
        gather(0)
        scatter(0)
        nc.vector.tensor_copy(**cast_views(2))
        nc.vector.tensor_copy(**cast_views(3))
        quantize_h(2)
        nc.scalar.activation(out=z[2][:], in_=product(2, 0, S)[:], func=ACT.Copy)
        quantize_h(3)
        penalty(drop[1], counts[1])
        gather(1)
        scatter(1)
        nc.gpsimd.tensor_scalar(
            out=drop_last[:], in0=counts_last[:], scalar1=-0.3, scalar2=-0.2, op0=ALU.mult, op1=ALU.add
        )
        logits(3)
        row_max(0)
        exponential(0)
        plain_gather(3)
        gather(2)
        scatter(2)
        fused_scatter(3)
        inverse(0)
        row_max(1)
        exponential(1)
        row_max(3)
        exponential(3)
        nc.gpsimd.tensor_scalar(
            out=prob[0][:], in0=e[0][:], scalar1=inv[0][:], scalar2=0.0, op0=ALU.mult, op1=ALU.add
        )
        nc.sync.dma_start(out=out[0:P, :], in_=prob[0][:])
        row_max(2)
        exponential(2)
        inverse(1)
        normalise(1, 0)
        inverse(3)
        normalise(3, 0)
        inverse(2)
        normalise(2, P)
